import numpy as np
import ml_dtypes


def mxq(x, axis, fmt="e4m3"):
    dtype, down = {"e4m3": (ml_dtypes.float8_e4m3fn, 7), "e5m2": (ml_dtypes.float8_e5m2, 14)}[fmt]
    v = np.moveaxis(np.asarray(x, np.float32).astype(ml_dtypes.bfloat16).astype(np.float64), axis, -1)
    blocks = v.reshape(v.shape[:-1] + (-1, 32))
    amax = np.abs(blocks).max(-1, keepdims=True)
    byte = np.maximum(np.where(amax > 0, np.frexp(amax)[1] - 1 + 127, 0) - down, 1)
    scale = np.exp2(byte - 127.0)
    codes = (blocks / scale).astype(np.float32).astype(dtype).astype(np.float64)
    return np.moveaxis((codes * scale).reshape(v.shape), -1, axis)


WIDE = False


def mx_kscale(k):
    if not WIDE:
        return np.ones(k)
    levels = np.array([10, -10, 5, -5, 0])
    if k % 512:
        return np.exp2(np.random.permutation(np.resize(levels, k // 32))).repeat(32)
    a = np.empty((k // 512, 16))
    for p in range(k // 512):
        a[p, :8] = np.random.permutation(np.resize(levels, 8))
        for g in range(8):
            far = levels[np.abs(levels - a[p, g]) >= 10]
            a[p, g + 8] = far[np.random.randint(len(far))]
    return np.exp2(a.ravel()).repeat(32)


def f64(x):
    return np.asarray(x).astype(np.float64)


def striped(idx):
    return np.tile(idx.reshape(-1, 16).T, (8, 1)).astype(np.uint16)


def unstriped(offs):
    return offs[:16].T.reshape(-1).astype(np.int64)


E2M1 = np.array([0.0, 0.5, 1.0, 1.5, 2.0, 3.0, 4.0, 6.0, -0.0, -0.5, -1.0, -1.5, -2.0, -3.0, -4.0, -6.0])


def pack_weight(w, fmt):
    k, n = w.shape
    w = f64(np.asarray(w, np.float32).astype(ml_dtypes.bfloat16)).reshape(k // 32, 32, n)
    amax = np.abs(w).max(1)
    if fmt == "e4m3":
        byte = np.frexp(amax)[1] - 1 + 127 - 7
    else:
        mant, ex = np.frexp(amax / 6.0)
        byte = np.where(mant > 0.5, ex, ex - 1) + 127
    byte = np.clip(np.where(amax > 0, byte, 1), 1, 254)
    scaled = (w * np.exp2(127.0 - byte)[:, None, :]).reshape(k, n).astype(np.float32)
    by_word = np.ascontiguousarray(scaled.reshape(k // 512, 128, 4, n).transpose(0, 1, 3, 2))
    if fmt == "e4m3":
        words = by_word.astype(ml_dtypes.float8_e4m3fn).view(np.uint8)
    else:
        c = by_word.astype(ml_dtypes.float4_e2m1fn).view(np.uint8) & 0xF
        words = (c[..., 0::2] | (c[..., 1::2] << 4)).reshape(k // 512, 128, 2 * n)
    return np.ascontiguousarray(words), np.ascontiguousarray(byte.astype(np.uint8).reshape(k // 512, 16, n))


def unpack_weight(words, scales, fmt):
    g, _, n = scales.shape
    words = np.ascontiguousarray(words).reshape(g, 128, n, -1)
    if fmt == "e4m3":
        vals = words.view(ml_dtypes.float8_e4m3fn).astype(np.float64)
    else:
        nib = np.empty((g, 128, n, 4), np.uint8)
        nib[..., 0::2] = words & 0xF
        nib[..., 1::2] = words >> 4
        vals = E2M1[nib]
    vals = vals * np.repeat(np.exp2(scales.astype(np.float64) - 127.0), 8, axis=1)[..., None]
    return vals.transpose(0, 1, 3, 2).reshape(g * 512, n)


def gelu(v):
    return 0.5 * v * (1.0 + np.tanh(np.sqrt(2.0 / np.pi) * (v + 0.044715 * v**3)))


K, T, S, H, N = 1536, 2048, 1024, 512, 384

def setup_inputs():
    n = np.random.standard_normal
    s = mx_kscale(K)[:, None]
    u = mx_kscale(H)[:, None]
    tab_words, tab_scales = pack_weight(n((K, T)) * s, "e4m3")
    w1 = (n((K, H)) / np.sqrt(K) / s * u.T).astype(np.float32)
    gT = (n((H, T)) * u).astype(np.float32)
    w4_words, w4_scales = pack_weight(0.7 * n((H, N)) / np.sqrt(H) / u, "e2m1")
    b = (0.5 * n(N)).astype(np.float32)
    offs = striped(np.random.permutation(T)[:S])
    return {"tab_words": tab_words, "tab_scales": tab_scales, "offs": offs, "w1": w1,
            "gT": gT, "w4_words": w4_words, "w4_scales": w4_scales, "b": b}

def reference(tab_words, tab_scales, offs, w1, gT, w4_words, w4_scales, b):
    v = unpack_weight(tab_words, tab_scales, "e4m3")[:, unstriped(offs)]
    g = f64(gT)[:, unstriped(offs)]
    w1q = mxq(f64(w1), 0, "e4m3")
    w4 = unpack_weight(w4_words, w4_scales, "e2m1")
    A = w1q.T @ v
    h = np.abs(A - g)
    hq = mxq(h, 0, "e4m3")
    y = w4.T @ hq
    return np.tanh(y + f64(b)[:, None])

@@ -1,0 +1,183 @@
+from contextlib import ExitStack
+
+import concourse.mybir as mybir
+
+K, T, S, H, N = 1536, 2048, 1024, 512, 384
+FLOPS = 2 * K * H * S + 2 * H * N * S
+
+F32 = mybir.dt.float32
+BF16 = mybir.dt.bfloat16
+I32 = mybir.dt.int32
+U32 = mybir.dt.uint32
+U16 = mybir.dt.uint16
+U8 = mybir.dt.uint8
+FP8X4 = mybir.dt.float8_e4m3fn_x4
+FP4X4 = mybir.dt.float4_e2m1fn_x4
+ACT = mybir.ActivationFunctionType
+ALU = mybir.AluOpType
+
+P = 128
+PACK = 4
+K_PASS = P * PACK
+PASSES = K // K_PASS
+N_TILES = N // P
+CHUNK = 128
+GATHER = 256
+GROUPS = (256, 256, 256, 128, 128)
+
+
+def tile_list_keypoint_patch_change_kernel(tc, tab_words, tab_scales, offs, w1, gT, w4_words, w4_scales, b, out):
+    nc = tc.nc
+    with ExitStack() as ctx:
+        keep = ctx.enter_context(tc.tile_pool(name="keep", bufs=1))
+        ring = ctx.enter_context(tc.tile_pool(name="ring", bufs=8))
+        psum = ctx.enter_context(tc.psum_pool(name="psum", bufs=1))
+
+        offsets = keep.tile([P, S // 16], U16, name="offsets")
+        nc.sync.dma_start(offsets[:], offs)
+
+        def picks(first, count):
+            return offsets[:, first // 16 : (first + count) // 16]
+
+        tab_sc = keep.tile([P, T // 4], I32, name="tab_sc", align_bytes=64)
+        w4_sc = keep.tile([P, N // 4], I32, name="w4_sc", align_bytes=64)
+        zero = keep.tile([P, 1], F32, name="zero")
+        no_bias = keep.tile([P, 1], F32, name="no_bias")
+        nc.vector.memset(tab_sc[:], 0)
+        nc.vector.memset(w4_sc[:], 0)
+        nc.vector.memset(zero[:], 0.0)
+        nc.scalar.activation(out=no_bias[:], in_=zero[:], func=ACT.Tanh)
+
+        w_raw = [keep.tile([P, PACK, H], F32, name=f"w_raw{a}") for a in range(PASSES)]
+        for a in range(PASSES):
+            nc.sync.dma_start(
+                out=w_raw[a][:], in_=w1[a * K_PASS : (a + 1) * K_PASS, :].rearrange("(p j) c -> p j c", j=PACK)
+            )
+            if a == 1:
+                for q in range(4):
+                    nc.sync.dma_start(
+                        out=tab_sc[32 * q : 32 * q + 4 * PASSES, :],
+                        in_=tab_scales[:, 4 * q : 4 * q + 4, :].bitcast(I32),
+                    )
+        tab = [keep.tile([P, T], I32, name=f"tab{a}") for a in range(PASSES)]
+        for a in range(PASSES):
+            nc.sync.dma_start(out=tab[a][:], in_=tab_words[a].rearrange("p t i -> p (t i)").bitcast(I32))
+        g_planes = gT.rearrange("(p t) n -> t p n", t=PACK)
+        g_all = [keep.tile([P, T], F32, name=f"g_all{t}") for t in range(PACK)]
+        for t in range(PACK):
+            nc.sync.dma_start(out=g_all[t][:], in_=g_planes[t])
+        w4_codes = keep.tile([P, 2 * N // 4], I32, name="w4_codes", align_bytes=64)
+        nc.sync.dma_start(out=w4_codes[:], in_=w4_words[0].bitcast(I32))
+        for q in range(4):
+            nc.sync.dma_start(
+                out=w4_sc[32 * q : 32 * q + 4, :], in_=w4_scales[0, 4 * q : 4 * q + 4, :].bitcast(I32)
+            )
+        bias = keep.tile([P, N_TILES], F32, name="bias")
+        with nc.allow_non_contiguous_dma(reason="one bias value a partition"):
+            nc.sync.dma_start(out=bias[:], in_=b.rearrange("(c p) -> p c", p=P))
+
+
+        v_sc = keep.tile([P, S], U8, name="v_sc", align_bytes=64)
+        nc.vector.tensor_copy(out=v_sc[:], in_=tab_sc[:].bitcast(U8).indirect(offsets[:]))
+
+        w_codes = keep.tile([P, PASSES, H], U32, name="w_codes", align_bytes=64)
+        w_sc = keep.tile([P, PASSES, H], U8, name="w_sc", align_bytes=64)
+        for a in range(PASSES):
+            w_bf = keep.tile([P, PACK, P, PACK], BF16, name=f"w_bf{a}", align_bytes=64)
+            src = w_raw[a][:].rearrange("p j (m t) -> p t m j", t=PACK)
+            nc.vector.tensor_copy(out=w_bf[:, 0:2], in_=src[:, 0:2])
+            nc.scalar.copy(out=w_bf[:, 2:4], in_=src[:, 2:4])
+            nc.vector.quantize_mx(
+                out=w_codes[:, a, :].bitcast(FP8X4),
+                scales=w_sc[:, a, :],
+                in_=w_bf[:].rearrange("p t m j -> p (t m j)"),
+            )
+
+        v_codes = keep.tile([P, PASSES, S], U32, name="v_codes", align_bytes=64)
+        for a in range(PASSES):
+            pieces = 2 if a == PASSES - 1 else 1
+            width = S // pieces
+            for i in range(pieces):
+                nc.vector.tensor_copy(
+                    out=v_codes[:, a, i * width : (i + 1) * width],
+                    in_=tab[a][:].bitcast(U32).indirect(picks(i * width, width)),
+                )
+
+        g_pick = keep.tile([P, PACK, S], F32, name="g_pick")
+        for t in range(PACK - 1):
+            nc.vector.tensor_copy(out=g_pick[:, t, :], in_=g_all[t][:].indirect(offsets[:]))
+
+        h_bf = keep.tile([P, S, PACK], BF16, name="h_bf", align_bytes=64)
+        h_codes = keep.tile([P, S], U32, name="h_codes", align_bytes=64)
+        h_sc = keep.tile([P, S], U8, name="h_sc", align_bytes=64)
+        result = keep.tile([P, N_TILES, S], F32, name="result")
+        out_view = out.rearrange("(c p) j -> p c j", p=P)
+        w4_bytes = w4_codes[:].bitcast(U8)
+        w4_sc_bytes = w4_sc[:].bitcast(U8)
+
+        def first_product(c):
+            cols = slice(c * CHUNK, (c + 1) * CHUNK)
+            acc = psum.tile([P, PACK, CHUNK], F32, name=f"acc{c}")
+            for t in range(PACK):
+                for a in range(PASSES):
+                    nc.tensor.matmul_mx(
+                        out=acc[:, t, :],
+                        lhsT=w_codes[:, a, t * P : (t + 1) * P].bitcast(FP8X4),
+                        lhsT_scale=w_sc[:, a, t * P : (t + 1) * P],
+                        rhs=v_codes[:, a, cols].bitcast(FP8X4),
+                        rhs_scale=v_sc[4 * a : P, cols],
+                        start=(a == 0),
+                        stop=(a == PASSES - 1),
+                    )
+            return acc
+
+        def change(c, acc):
+            cols = slice(c * CHUNK, (c + 1) * CHUNK)
+            if (c * CHUNK) % GATHER == 0:
+                nc.vector.tensor_copy(
+                    out=g_pick[:, PACK - 1, c * CHUNK : c * CHUNK + GATHER],
+                    in_=g_all[PACK - 1][:].indirect(picks(c * CHUNK, GATHER)),
+                )
+            diff = ring.tile([P, PACK, CHUNK], F32, name="diff")
+            nc.vector.tensor_tensor(out=diff[:], in0=acc[:], in1=g_pick[:, :, cols], op=ALU.subtract)
+            nc.scalar.activation(
+                out=h_bf[:, cols, :].rearrange("p (c i) t -> p c t i", i=4),
+                in_=diff[:].rearrange("p t (c i) -> p c t i", i=4),
+                func=ACT.Abs,
+                bias=no_bias[:],
+            )
+
+        def read_out(accs, first, width):
+            cols = slice(first, first + width)
+            nc.vector.quantize_mx(
+                out=h_codes[:, cols].bitcast(FP8X4),
+                scales=h_sc[:, cols],
+                in_=h_bf[:, cols, :].rearrange("p j t -> p (j t)"),
+            )
+            ys = []
+            for n in range(N_TILES):
+                bank, start = divmod(n * width, PACK * CHUNK)
+                y = accs[first // CHUNK + bank][:].rearrange("p t j -> p (t j)")[:, start : start + width]
+                nc.tensor.matmul_mx(
+                    out=y,
+                    lhsT=w4_bytes[:, 2 * P * n : 2 * P * (n + 1)].bitcast(FP4X4),
+                    lhsT_scale=w4_sc_bytes[:, P * n : P * (n + 1)],
+                    rhs=h_codes[:, cols].bitcast(FP8X4),
+                    rhs_scale=h_sc[:, cols],
+                    start=True,
+                    stop=True,
+                )
+                ys.append(y)
+            for n in range(N_TILES):
+                nc.scalar.activation(out=result[:, n, cols], in_=ys[n], func=ACT.Tanh, bias=bias[:, n : n + 1])
+            nc.sync.dma_start(out=out_view[:, :, cols], in_=result[:, :, cols])
+
+        chunks = S // CHUNK
+        starts = [sum(GROUPS[:i]) for i in range(len(GROUPS))]
+        accs = [first_product(c) for c in range(chunks)]
+        for c in range(chunks + 1):
+            if c < chunks:
+                change(c, accs[c])
+            for first, width in zip(starts, GROUPS):
+                if first + width == c * CHUNK:
+                    read_out(accs, first, width)

@@ -21,16 +21,15 @@ PACK = 4
 K_PASS = P * PACK
 PASSES = K // K_PASS
 N_TILES = N // P
-CHUNK = 128
-GATHER = 256
-GROUPS = (256, 256, 256, 128, 128)
+BANK = 512
+CHUNK = 256
+CHUNKS = S // CHUNK
 
 
 def tile_list_keypoint_patch_change_kernel(tc, tab_words, tab_scales, offs, w1, gT, w4_words, w4_scales, b, out):
     nc = tc.nc
     with ExitStack() as ctx:
         keep = ctx.enter_context(tc.tile_pool(name="keep", bufs=1))
-        ring = ctx.enter_context(tc.tile_pool(name="ring", bufs=8))
         psum = ctx.enter_context(tc.psum_pool(name="psum", bufs=1))
 
         offsets = keep.tile([P, S // 16], U16, name="offsets")
@@ -43,40 +42,52 @@ def tile_list_keypoint_patch_change_kernel(tc, tab_words, tab_scales, offs, w1, 
         w4_sc = keep.tile([P, N // 4], I32, name="w4_sc", align_bytes=64)
         zero = keep.tile([P, 1], F32, name="zero")
         no_bias = keep.tile([P, 1], F32, name="no_bias")
-        nc.vector.memset(tab_sc[:], 0)
+        nc.gpsimd.memset(tab_sc[:], 0)
         nc.vector.memset(w4_sc[:], 0)
         nc.vector.memset(zero[:], 0.0)
         nc.scalar.activation(out=no_bias[:], in_=zero[:], func=ACT.Tanh)
 
+        def load_tab_scales():
+            for q in range(4):
+                nc.gpsimd.dma_start(
+                    out=tab_sc[32 * q : 32 * q + 4 * PASSES, :],
+                    in_=tab_scales[:, 4 * q : 4 * q + 4, :].bitcast(I32),
+                )
+
         w_raw = [keep.tile([P, PACK, H], F32, name=f"w_raw{a}") for a in range(PASSES)]
+        tab = [keep.tile([P, T], I32, name=f"tab{a}") for a in range(PASSES)]
+
+        def load_tab(a):
+            nc.sync.dma_start(out=tab[a][:], in_=tab_words[a].rearrange("p t i -> p (t i)").bitcast(I32))
+
+        load_tab_scales()
+        load_tab(0)
+        w4_codes = keep.tile([P, 2 * N // 4], I32, name="w4_codes", align_bytes=64)
+        nc.scalar.dma_start(out=w4_codes[:], in_=w4_words[0].bitcast(I32))
+        for q in range(4):
+            nc.scalar.dma_start(out=w4_sc[32 * q : 32 * q + 4, :], in_=w4_scales[0, 4 * q : 4 * q + 4, :].bitcast(I32))
         for a in range(PASSES):
             nc.sync.dma_start(
                 out=w_raw[a][:], in_=w1[a * K_PASS : (a + 1) * K_PASS, :].rearrange("(p j) c -> p j c", j=PACK)
             )
-            if a == 1:
-                for q in range(4):
-                    nc.sync.dma_start(
-                        out=tab_sc[32 * q : 32 * q + 4 * PASSES, :],
-                        in_=tab_scales[:, 4 * q : 4 * q + 4, :].bitcast(I32),
-                    )
-        tab = [keep.tile([P, T], I32, name=f"tab{a}") for a in range(PASSES)]
-        for a in range(PASSES):
-            nc.sync.dma_start(out=tab[a][:], in_=tab_words[a].rearrange("p t i -> p (t i)").bitcast(I32))
+        for a in range(1, PASSES):
+            load_tab(a)
         g_planes = gT.rearrange("(p t) n -> t p n", t=PACK)
         g_all = [keep.tile([P, T], F32, name=f"g_all{t}") for t in range(PACK)]
         for t in range(PACK):
             nc.sync.dma_start(out=g_all[t][:], in_=g_planes[t])
-        w4_codes = keep.tile([P, 2 * N // 4], I32, name="w4_codes", align_bytes=64)
-        nc.sync.dma_start(out=w4_codes[:], in_=w4_words[0].bitcast(I32))
-        for q in range(4):
-            nc.sync.dma_start(
-                out=w4_sc[32 * q : 32 * q + 4, :], in_=w4_scales[0, 4 * q : 4 * q + 4, :].bitcast(I32)
-            )
         bias = keep.tile([P, N_TILES], F32, name="bias")
         with nc.allow_non_contiguous_dma(reason="one bias value a partition"):
             nc.sync.dma_start(out=bias[:], in_=b.rearrange("(c p) -> p c", p=P))
 
+        v_codes = keep.tile([P, PASSES, S], U32, name="v_codes", align_bytes=64)
 
+        def gather_words(a, first, count):
+            nc.vector.tensor_copy(
+                out=v_codes[:, a, first : first + count], in_=tab[a][:].bitcast(U32).indirect(picks(first, count))
+            )
+
+        gather_words(0, 0, S)
         v_sc = keep.tile([P, S], U8, name="v_sc", align_bytes=64)
         nc.vector.tensor_copy(out=v_sc[:], in_=tab_sc[:].bitcast(U8).indirect(offsets[:]))
 
@@ -84,29 +95,49 @@ def tile_list_keypoint_patch_change_kernel(tc, tab_words, tab_scales, offs, w1, 
         w_sc = keep.tile([P, PASSES, H], U8, name="w_sc", align_bytes=64)
         for a in range(PASSES):
             w_bf = keep.tile([P, PACK, P, PACK], BF16, name=f"w_bf{a}", align_bytes=64)
-            src = w_raw[a][:].rearrange("p j (m t) -> p t m j", t=PACK)
-            nc.vector.tensor_copy(out=w_bf[:, 0:2], in_=src[:, 0:2])
-            nc.scalar.copy(out=w_bf[:, 2:4], in_=src[:, 2:4])
+            dst = w_bf[:].rearrange("p t m j -> p m j t")
+            src = w_raw[a][:].rearrange("p j (m t) -> p m j t", t=PACK)
+            if a == PASSES - 1:
+                nc.vector.tensor_copy(out=dst[:, 0 : P // 2], in_=src[:, 0 : P // 2])
+                nc.scalar.copy(out=dst[:, P // 2 : P], in_=src[:, P // 2 : P])
+            else:
+                nc.scalar.copy(out=dst, in_=src)
             nc.vector.quantize_mx(
                 out=w_codes[:, a, :].bitcast(FP8X4),
                 scales=w_sc[:, a, :],
                 in_=w_bf[:].rearrange("p t m j -> p (t m j)"),
             )
 
-        v_codes = keep.tile([P, PASSES, S], U32, name="v_codes", align_bytes=64)
+        def product(acc, t, a, cols):
+            nc.tensor.matmul_mx(
+                out=acc,
+                lhsT=w_codes[:, a, t * P : (t + 1) * P].bitcast(FP8X4),
+                lhsT_scale=w_sc[:, a, t * P : (t + 1) * P],
+                rhs=v_codes[:, a, cols].bitcast(FP8X4),
+                rhs_scale=v_sc[4 * a : P, cols],
+                start=(a == 0),
+                stop=(a == PASSES - 1),
+            )
+
+        halves = [slice(0, BANK), slice(BANK, S)]
+        early = [[psum.tile([P, BANK], F32, name=f"early{t}_{u}") for u in range(2)] for t in range(2)]
+        late = [psum.tile([P, 2, CHUNK], F32, name=f"late{c}") for c in range(CHUNKS)]
         for a in range(PASSES):
-            pieces = 2 if a == PASSES - 1 else 1
-            width = S // pieces
-            for i in range(pieces):
-                nc.vector.tensor_copy(
-                    out=v_codes[:, a, i * width : (i + 1) * width],
-                    in_=tab[a][:].bitcast(U32).indirect(picks(i * width, width)),
-                )
+            if a == 1:
+                gather_words(a, 0, S)
+            if a == 2:
+                gather_words(a, 0, BANK)
+                gather_words(a, BANK, BANK)
+            for u in range(2):
+                for t in range(2):
+                    product(early[t][u][:], t, a, halves[u])
+        for c in range(CHUNKS):
+            for t in range(2):
+                for a in range(PASSES):
+                    product(late[c][:, t, :], 2 + t, a, slice(c * CHUNK, (c + 1) * CHUNK))
 
         g_pick = keep.tile([P, PACK, S], F32, name="g_pick")
-        for t in range(PACK - 1):
-            nc.vector.tensor_copy(out=g_pick[:, t, :], in_=g_all[t][:].indirect(offsets[:]))
-
+        diff = keep.tile([P, PACK, S], F32, name="diff")
         h_bf = keep.tile([P, S, PACK], BF16, name="h_bf", align_bytes=64)
         h_codes = keep.tile([P, S], U32, name="h_codes", align_bytes=64)
         h_sc = keep.tile([P, S], U8, name="h_sc", align_bytes=64)
@@ -115,51 +146,45 @@ def tile_list_keypoint_patch_change_kernel(tc, tab_words, tab_scales, offs, w1, 
         w4_bytes = w4_codes[:].bitcast(U8)
         w4_sc_bytes = w4_sc[:].bitcast(U8)
 
-        def first_product(c):
-            cols = slice(c * CHUNK, (c + 1) * CHUNK)
-            acc = psum.tile([P, PACK, CHUNK], F32, name=f"acc{c}")
-            for t in range(PACK):
-                for a in range(PASSES):
-                    nc.tensor.matmul_mx(
-                        out=acc[:, t, :],
-                        lhsT=w_codes[:, a, t * P : (t + 1) * P].bitcast(FP8X4),
-                        lhsT_scale=w_sc[:, a, t * P : (t + 1) * P],
-                        rhs=v_codes[:, a, cols].bitcast(FP8X4),
-                        rhs_scale=v_sc[4 * a : P, cols],
-                        start=(a == 0),
-                        stop=(a == PASSES - 1),
-                    )
-            return acc
+        def gather_g(t, first, count):
+            nc.vector.tensor_copy(out=g_pick[:, t, first : first + count], in_=g_all[t][:].indirect(picks(first, count)))
 
-        def change(c, acc):
-            cols = slice(c * CHUNK, (c + 1) * CHUNK)
-            if (c * CHUNK) % GATHER == 0:
-                nc.vector.tensor_copy(
-                    out=g_pick[:, PACK - 1, c * CHUNK : c * CHUNK + GATHER],
-                    in_=g_all[PACK - 1][:].indirect(picks(c * CHUNK, GATHER)),
-                )
-            diff = ring.tile([P, PACK, CHUNK], F32, name="diff")
-            nc.vector.tensor_tensor(out=diff[:], in0=acc[:], in1=g_pick[:, :, cols], op=ALU.subtract)
+        def absolute(t0, cols):
             nc.scalar.activation(
-                out=h_bf[:, cols, :].rearrange("p (c i) t -> p c t i", i=4),
-                in_=diff[:].rearrange("p t (c i) -> p c t i", i=4),
+                out=h_bf[:, cols, t0 : t0 + 2].rearrange("p (c i) t -> p c t i", i=4),
+                in_=diff[:, t0 : t0 + 2, cols].rearrange("p t (c i) -> p c t i", i=4),
                 func=ACT.Abs,
                 bias=no_bias[:],
             )
 
-        def read_out(accs, first, width):
+        for t in range(3):
+            gather_g(t, 0, S)
+            if t > 0:
+                for u in range(2):
+                    nc.vector.tensor_tensor(
+                        out=diff[:, t - 1, halves[u]], in0=early[t - 1][u][:], in1=g_pick[:, t - 1, halves[u]], op=ALU.subtract
+                    )
+        for u in range(2):
+            absolute(0, halves[u])
+
+        def change(first, width):
+            cols = slice(first, first + width)
+            c, start = divmod(first, CHUNK)
+            nc.vector.tensor_tensor(
+                out=diff[:, 2:4, cols], in0=late[c][:, :, start : start + width], in1=g_pick[:, 2:4, cols], op=ALU.subtract
+            )
+            absolute(2, cols)
+
+        def read_out(first, width, ys):
             cols = slice(first, first + width)
             nc.vector.quantize_mx(
                 out=h_codes[:, cols].bitcast(FP8X4),
                 scales=h_sc[:, cols],
                 in_=h_bf[:, cols, :].rearrange("p j t -> p (j t)"),
             )
-            ys = []
             for n in range(N_TILES):
-                bank, start = divmod(n * width, PACK * CHUNK)
-                y = accs[first // CHUNK + bank][:].rearrange("p t j -> p (t j)")[:, start : start + width]
                 nc.tensor.matmul_mx(
-                    out=y,
+                    out=ys[n],
                     lhsT=w4_bytes[:, 2 * P * n : 2 * P * (n + 1)].bitcast(FP4X4),
                     lhsT_scale=w4_sc_bytes[:, P * n : P * (n + 1)],
                     rhs=h_codes[:, cols].bitcast(FP8X4),
@@ -167,17 +192,22 @@ def tile_list_keypoint_patch_change_kernel(tc, tab_words, tab_scales, offs, w1, 
                     start=True,
                     stop=True,
                 )
-                ys.append(y)
             for n in range(N_TILES):
                 nc.scalar.activation(out=result[:, n, cols], in_=ys[n], func=ACT.Tanh, bias=bias[:, n : n + 1])
             nc.sync.dma_start(out=out_view[:, :, cols], in_=result[:, :, cols])
 
-        chunks = S // CHUNK
-        starts = [sum(GROUPS[:i]) for i in range(len(GROUPS))]
-        accs = [first_product(c) for c in range(chunks)]
-        for c in range(chunks + 1):
-            if c < chunks:
-                change(c, accs[c])
-            for first, width in zip(starts, GROUPS):
-                if first + width == c * CHUNK:
-                    read_out(accs, first, width)
+        free = [early[t][u] for t in range(2) for u in range(2)]
+        half = CHUNK // 2
+        groups = [(c * CHUNK, CHUNK, [free[c][:, 0:CHUNK], free[c][:, CHUNK:BANK], late[c][:, 0, :]]) for c in range(CHUNKS - 1)]
+        last = (CHUNKS - 1) * CHUNK
+        tail_bank = late[CHUNKS - 1][:].rearrange("p t j -> p (t j)")
+        groups.append((last, half, [free[CHUNKS - 1][:, n * half : (n + 1) * half] for n in range(N_TILES)]))
+        groups.append((last + half, half, [tail_bank[:, n * half : (n + 1) * half] for n in range(N_TILES)]))
+        gather_g(3, 0, CHUNK)
+        for i, (first, width, ys) in enumerate(groups):
+            if first % CHUNK == 0 and first + CHUNK < S:
+                gather_g(3, first + CHUNK, CHUNK)
+            change(first, width)
+            if i > 0:
+                read_out(*groups[i - 1])
+        read_out(*groups[-1])

@@ -49,7 +49,7 @@ def tile_list_keypoint_patch_change_kernel(tc, tab_words, tab_scales, offs, w1, 
 
         def load_tab_scales():
             for q in range(4):
-                nc.gpsimd.dma_start(
+                nc.sync.dma_start(
                     out=tab_sc[32 * q : 32 * q + 4 * PASSES, :],
                     in_=tab_scales[:, 4 * q : 4 * q + 4, :].bitcast(I32),
                 )
@@ -60,25 +60,25 @@ def tile_list_keypoint_patch_change_kernel(tc, tab_words, tab_scales, offs, w1, 
         def load_tab(a):
             nc.sync.dma_start(out=tab[a][:], in_=tab_words[a].rearrange("p t i -> p (t i)").bitcast(I32))
 
-        load_tab_scales()
         load_tab(0)
-        w4_codes = keep.tile([P, 2 * N // 4], I32, name="w4_codes", align_bytes=64)
-        nc.scalar.dma_start(out=w4_codes[:], in_=w4_words[0].bitcast(I32))
-        for q in range(4):
-            nc.scalar.dma_start(out=w4_sc[32 * q : 32 * q + 4, :], in_=w4_scales[0, 4 * q : 4 * q + 4, :].bitcast(I32))
+        load_tab_scales()
         for a in range(PASSES):
             nc.sync.dma_start(
                 out=w_raw[a][:], in_=w1[a * K_PASS : (a + 1) * K_PASS, :].rearrange("(p j) c -> p j c", j=PACK)
             )
         for a in range(1, PASSES):
             load_tab(a)
+        w4_codes = keep.tile([P, 2 * N // 4], I32, name="w4_codes", align_bytes=64)
+        nc.sync.dma_start(out=w4_codes[:], in_=w4_words[0].bitcast(I32))
+        for q in range(4):
+            nc.sync.dma_start(out=w4_sc[32 * q : 32 * q + 4, :], in_=w4_scales[0, 4 * q : 4 * q + 4, :].bitcast(I32))
+        bias = keep.tile([P, N_TILES], F32, name="bias")
+        with nc.allow_non_contiguous_dma(reason="one bias value a partition"):
+            nc.sync.dma_start(out=bias[:], in_=b.rearrange("(c p) -> p c", p=P))
         g_planes = gT.rearrange("(p t) n -> t p n", t=PACK)
         g_all = [keep.tile([P, T], F32, name=f"g_all{t}") for t in range(PACK)]
         for t in range(PACK):
             nc.sync.dma_start(out=g_all[t][:], in_=g_planes[t])
-        bias = keep.tile([P, N_TILES], F32, name="bias")
-        with nc.allow_non_contiguous_dma(reason="one bias value a partition"):
-            nc.sync.dma_start(out=bias[:], in_=b.rearrange("(c p) -> p c", p=P))
 
         v_codes = keep.tile([P, PASSES, S], U32, name="v_codes", align_bytes=64)
 
@@ -97,7 +97,7 @@ def tile_list_keypoint_patch_change_kernel(tc, tab_words, tab_scales, offs, w1, 
             w_bf = keep.tile([P, PACK, P, PACK], BF16, name=f"w_bf{a}", align_bytes=64)
             dst = w_bf[:].rearrange("p t m j -> p m j t")
             src = w_raw[a][:].rearrange("p j (m t) -> p m j t", t=PACK)
-            if a == PASSES - 1:
+            if a > 0:
                 nc.vector.tensor_copy(out=dst[:, 0 : P // 2], in_=src[:, 0 : P // 2])
                 nc.scalar.copy(out=dst[:, P // 2 : P], in_=src[:, P // 2 : P])
             else:
@@ -136,8 +136,11 @@ def tile_list_keypoint_patch_change_kernel(tc, tab_words, tab_scales, offs, w1, 
                 for a in range(PASSES):
                     product(late[c][:, t, :], 2 + t, a, slice(c * CHUNK, (c + 1) * CHUNK))
 
-        g_pick = keep.tile([P, PACK, S], F32, name="g_pick")
-        diff = keep.tile([P, PACK, S], F32, name="diff")
+        work = keep.tile([P, PACK * S + BANK], F32, name="work")
+        g_pick = work[:, 0 : PACK * S].rearrange("p (t j) -> p t j", t=PACK)
+        borrowed = work[:, PACK * S - BANK :].rearrange("p (t j) -> p t j", t=2)
+        diff_early = keep.tile([P, 2, S], F32, name="diff_early")
+        diff_late = keep.tile([P, 2, BANK], F32, name="diff_late")
         h_bf = keep.tile([P, S, PACK], BF16, name="h_bf", align_bytes=64)
         h_codes = keep.tile([P, S], U32, name="h_codes", align_bytes=64)
         h_sc = keep.tile([P, S], U8, name="h_sc", align_bytes=64)
@@ -149,31 +152,36 @@ def tile_list_keypoint_patch_change_kernel(tc, tab_words, tab_scales, offs, w1, 
         def gather_g(t, first, count):
             nc.vector.tensor_copy(out=g_pick[:, t, first : first + count], in_=g_all[t][:].indirect(picks(first, count)))
 
-        def absolute(t0, cols):
+        def absolute(t0, cols, diff):
             nc.scalar.activation(
                 out=h_bf[:, cols, t0 : t0 + 2].rearrange("p (c i) t -> p c t i", i=4),
-                in_=diff[:, t0 : t0 + 2, cols].rearrange("p t (c i) -> p c t i", i=4),
+                in_=diff.rearrange("p t (c i) -> p c t i", i=4),
                 func=ACT.Abs,
                 bias=no_bias[:],
             )
 
-        for t in range(3):
-            gather_g(t, 0, S)
-            if t > 0:
-                for u in range(2):
-                    nc.vector.tensor_tensor(
-                        out=diff[:, t - 1, halves[u]], in0=early[t - 1][u][:], in1=g_pick[:, t - 1, halves[u]], op=ALU.subtract
-                    )
+        a_early = keep.tile([P, 2, S], F32, name="a_early")
+        for t in range(2):
+            for u in range(2):
+                nc.scalar.copy(out=a_early[:, t, halves[u]], in_=early[t][u][:])
+        for t in range(2):
+            for u in range(2):
+                gather_g(t, u * BANK, BANK)
+                nc.gpsimd.tensor_tensor(
+                    out=diff_early[:, t, halves[u]], in0=a_early[:, t, halves[u]], in1=g_pick[:, t, halves[u]], op=ALU.subtract
+                )
         for u in range(2):
-            absolute(0, halves[u])
+            absolute(0, halves[u], diff_early[:, :, halves[u]])
+        gather_g(2, 0, S)
 
         def change(first, width):
             cols = slice(first, first + width)
             c, start = divmod(first, CHUNK)
+            diff = borrowed[:, :, cols] if first < BANK else diff_late[:, :, first - BANK : first - BANK + width]
             nc.vector.tensor_tensor(
-                out=diff[:, 2:4, cols], in0=late[c][:, :, start : start + width], in1=g_pick[:, 2:4, cols], op=ALU.subtract
+                out=diff, in0=late[c][:, :, start : start + width], in1=g_pick[:, 2:4, cols], op=ALU.subtract
             )
-            absolute(2, cols)
+            absolute(2, cols, diff)
 
         def read_out(first, width, ys):
             cols = slice(first, first + width)
@@ -203,11 +211,17 @@ def tile_list_keypoint_patch_change_kernel(tc, tab_words, tab_scales, offs, w1, 
         tail_bank = late[CHUNKS - 1][:].rearrange("p t j -> p (t j)")
         groups.append((last, half, [free[CHUNKS - 1][:, n * half : (n + 1) * half] for n in range(N_TILES)]))
         groups.append((last + half, half, [tail_bank[:, n * half : (n + 1) * half] for n in range(N_TILES)]))
-        gather_g(3, 0, CHUNK)
-        for i, (first, width, ys) in enumerate(groups):
-            if first % CHUNK == 0 and first + CHUNK < S:
-                gather_g(3, first + CHUNK, CHUNK)
-            change(first, width)
-            if i > 0:
-                read_out(*groups[i - 1])
-        read_out(*groups[-1])
+        gather_g(3, 0 * CHUNK, CHUNK)
+        gather_g(3, 1 * CHUNK, CHUNK)
+        change(*groups[0][0:2])
+        change(*groups[1][0:2])
+        read_out(*groups[0])
+        gather_g(3, 2 * CHUNK, CHUNK)
+        change(*groups[2][0:2])
+        read_out(*groups[1])
+        gather_g(3, 3 * CHUNK, CHUNK)
+        change(*groups[3][0:2])
+        change(*groups[4][0:2])
+        read_out(*groups[2])
+        read_out(*groups[3])
+        read_out(*groups[4])

@@ -21,6 +21,12 @@ PACK = 4
 K_PASS = P * PACK
 PASSES = K // K_PASS
 N_TILES = N // P
+QUADRANTS = 4
+ROWS = 4
+GROUP = 16
+LINE = 4
+PAIR = 2
+LAST = PACK - 1
 BANK = 512
 CHUNK = 256
 CHUNKS = S // CHUNK
@@ -32,11 +38,11 @@ def tile_list_keypoint_patch_change_kernel(tc, tab_words, tab_scales, offs, w1, 
         keep = ctx.enter_context(tc.tile_pool(name="keep", bufs=1))
         psum = ctx.enter_context(tc.psum_pool(name="psum", bufs=1))
 
-        offsets = keep.tile([P, S // 16], U16, name="offsets")
+        offsets = keep.tile([P, S // GROUP], U16, name="offsets")
         nc.sync.dma_start(offsets[:], offs)
 
         def picks(first, count):
-            return offsets[:, first // 16 : (first + count) // 16]
+            return offsets[:, first // GROUP : (first + count) // GROUP]
 
         tab_sc = keep.tile([P, T // 4], I32, name="tab_sc", align_bytes=64)
         w4_sc = keep.tile([P, N // 4], I32, name="w4_sc", align_bytes=64)
@@ -47,13 +53,6 @@ def tile_list_keypoint_patch_change_kernel(tc, tab_words, tab_scales, offs, w1, 
         nc.vector.memset(zero[:], 0.0)
         nc.scalar.activation(out=no_bias[:], in_=zero[:], func=ACT.Tanh)
 
-        def load_tab_scales():
-            for q in range(4):
-                nc.sync.dma_start(
-                    out=tab_sc[32 * q : 32 * q + 4 * PASSES, :],
-                    in_=tab_scales[:, 4 * q : 4 * q + 4, :].bitcast(I32),
-                )
-
         w_raw = [keep.tile([P, PACK, H], F32, name=f"w_raw{a}") for a in range(PASSES)]
         tab = [keep.tile([P, T], I32, name=f"tab{a}") for a in range(PASSES)]
 
@@ -61,33 +60,39 @@ def tile_list_keypoint_patch_change_kernel(tc, tab_words, tab_scales, offs, w1, 
             nc.sync.dma_start(out=tab[a][:], in_=tab_words[a].rearrange("p t i -> p (t i)").bitcast(I32))
 
         load_tab(0)
-        load_tab_scales()
+        for q in range(QUADRANTS):
+            nc.sync.dma_start(
+                out=tab_sc[32 * q : 32 * q + ROWS * PASSES, :],
+                in_=tab_scales[:, ROWS * q : ROWS * (q + 1), :].bitcast(I32),
+            )
         for a in range(PASSES):
             nc.sync.dma_start(
                 out=w_raw[a][:], in_=w1[a * K_PASS : (a + 1) * K_PASS, :].rearrange("(p j) c -> p j c", j=PACK)
             )
-        for a in range(1, PASSES):
-            load_tab(a)
+            if a + 1 < PASSES:
+                load_tab(a + 1)
+        g_planes = gT.rearrange("(p t) n -> t p n", t=PACK)
+        g_all = [keep.tile([P, T], F32, name=f"g_all{t}") for t in range(PACK)]
+        for t in range(PAIR):
+            nc.sync.dma_start(out=g_all[t][:], in_=g_planes[t])
         w4_codes = keep.tile([P, 2 * N // 4], I32, name="w4_codes", align_bytes=64)
         nc.sync.dma_start(out=w4_codes[:], in_=w4_words[0].bitcast(I32))
-        for q in range(4):
-            nc.sync.dma_start(out=w4_sc[32 * q : 32 * q + 4, :], in_=w4_scales[0, 4 * q : 4 * q + 4, :].bitcast(I32))
+        for q in range(QUADRANTS):
+            nc.sync.dma_start(
+                out=w4_sc[32 * q : 32 * q + ROWS, :], in_=w4_scales[0, ROWS * q : ROWS * (q + 1), :].bitcast(I32)
+            )
+        for t in range(PAIR, PACK):
+            nc.sync.dma_start(out=g_all[t][:], in_=g_planes[t])
         bias = keep.tile([P, N_TILES], F32, name="bias")
         with nc.allow_non_contiguous_dma(reason="one bias value a partition"):
             nc.sync.dma_start(out=bias[:], in_=b.rearrange("(c p) -> p c", p=P))
-        g_planes = gT.rearrange("(p t) n -> t p n", t=PACK)
-        g_all = [keep.tile([P, T], F32, name=f"g_all{t}") for t in range(PACK)]
-        for t in range(PACK):
-            nc.sync.dma_start(out=g_all[t][:], in_=g_planes[t])
 
         v_codes = keep.tile([P, PASSES, S], U32, name="v_codes", align_bytes=64)
 
-        def gather_words(a, first, count):
-            nc.vector.tensor_copy(
-                out=v_codes[:, a, first : first + count], in_=tab[a][:].bitcast(U32).indirect(picks(first, count))
-            )
+        def gather_words(a):
+            nc.vector.tensor_copy(out=v_codes[:, a, :], in_=tab[a][:].bitcast(U32).indirect(offsets[:]))
 
-        gather_words(0, 0, S)
+        gather_words(0)
         v_sc = keep.tile([P, S], U8, name="v_sc", align_bytes=64)
         nc.vector.tensor_copy(out=v_sc[:], in_=tab_sc[:].bitcast(U8).indirect(offsets[:]))
 
@@ -114,33 +119,30 @@ def tile_list_keypoint_patch_change_kernel(tc, tab_words, tab_scales, offs, w1, 
                 lhsT=w_codes[:, a, t * P : (t + 1) * P].bitcast(FP8X4),
                 lhsT_scale=w_sc[:, a, t * P : (t + 1) * P],
                 rhs=v_codes[:, a, cols].bitcast(FP8X4),
-                rhs_scale=v_sc[4 * a : P, cols],
+                rhs_scale=v_sc[ROWS * a : P, cols],
                 start=(a == 0),
                 stop=(a == PASSES - 1),
             )
 
         halves = [slice(0, BANK), slice(BANK, S)]
-        early = [[psum.tile([P, BANK], F32, name=f"early{t}_{u}") for u in range(2)] for t in range(2)]
-        late = [psum.tile([P, 2, CHUNK], F32, name=f"late{c}") for c in range(CHUNKS)]
+        early = [[psum.tile([P, BANK], F32, name=f"early{t}_{u}") for u in range(2)] for t in range(PAIR)]
+        late = [psum.tile([P, PAIR, CHUNK], F32, name=f"late{c}") for c in range(CHUNKS)]
         for a in range(PASSES):
-            if a == 1:
-                gather_words(a, 0, S)
-            if a == 2:
-                gather_words(a, 0, BANK)
-                gather_words(a, BANK, BANK)
+            if a > 0:
+                gather_words(a)
             for u in range(2):
-                for t in range(2):
+                for t in range(PAIR):
                     product(early[t][u][:], t, a, halves[u])
         for c in range(CHUNKS):
-            for t in range(2):
+            for t in range(PAIR):
                 for a in range(PASSES):
-                    product(late[c][:, t, :], 2 + t, a, slice(c * CHUNK, (c + 1) * CHUNK))
+                    product(late[c][:, t, :], PAIR + t, a, slice(c * CHUNK, (c + 1) * CHUNK))
 
         work = keep.tile([P, PACK * S + BANK], F32, name="work")
         g_pick = work[:, 0 : PACK * S].rearrange("p (t j) -> p t j", t=PACK)
-        borrowed = work[:, PACK * S - BANK :].rearrange("p (t j) -> p t j", t=2)
-        diff_early = keep.tile([P, 2, S], F32, name="diff_early")
-        diff_late = keep.tile([P, 2, BANK], F32, name="diff_late")
+        borrowed = work[:, PACK * S - BANK :].rearrange("p (t j) -> p t j", t=PAIR)
+        diff_early = keep.tile([P, PAIR, S], F32, name="diff_early")
+        diff_late = keep.tile([P, PAIR, BANK], F32, name="diff_late")
         h_bf = keep.tile([P, S, PACK], BF16, name="h_bf", align_bytes=64)
         h_codes = keep.tile([P, S], U32, name="h_codes", align_bytes=64)
         h_sc = keep.tile([P, S], U8, name="h_sc", align_bytes=64)
@@ -154,17 +156,17 @@ def tile_list_keypoint_patch_change_kernel(tc, tab_words, tab_scales, offs, w1, 
 
         def absolute(t0, cols, diff):
             nc.scalar.activation(
-                out=h_bf[:, cols, t0 : t0 + 2].rearrange("p (c i) t -> p c t i", i=4),
-                in_=diff.rearrange("p t (c i) -> p c t i", i=4),
+                out=h_bf[:, cols, t0 : t0 + PAIR].rearrange("p (c i) t -> p c t i", i=LINE),
+                in_=diff.rearrange("p t (c i) -> p c t i", i=LINE),
                 func=ACT.Abs,
                 bias=no_bias[:],
             )
 
-        a_early = keep.tile([P, 2, S], F32, name="a_early")
-        for t in range(2):
+        a_early = keep.tile([P, PAIR, S], F32, name="a_early")
+        for t in range(PAIR):
             for u in range(2):
                 nc.scalar.copy(out=a_early[:, t, halves[u]], in_=early[t][u][:])
-        for t in range(2):
+        for t in range(PAIR):
             for u in range(2):
                 gather_g(t, u * BANK, BANK)
                 nc.gpsimd.tensor_tensor(
@@ -172,16 +174,16 @@ def tile_list_keypoint_patch_change_kernel(tc, tab_words, tab_scales, offs, w1, 
                 )
         for u in range(2):
             absolute(0, halves[u], diff_early[:, :, halves[u]])
-        gather_g(2, 0, S)
+        gather_g(PAIR, 0, S)
 
         def change(first, width):
             cols = slice(first, first + width)
             c, start = divmod(first, CHUNK)
             diff = borrowed[:, :, cols] if first < BANK else diff_late[:, :, first - BANK : first - BANK + width]
             nc.vector.tensor_tensor(
-                out=diff, in0=late[c][:, :, start : start + width], in1=g_pick[:, 2:4, cols], op=ALU.subtract
+                out=diff, in0=late[c][:, :, start : start + width], in1=g_pick[:, PAIR:PACK, cols], op=ALU.subtract
             )
-            absolute(2, cols, diff)
+            absolute(PAIR, cols, diff)
 
         def read_out(first, width, ys):
             cols = slice(first, first + width)
@@ -200,28 +202,31 @@ def tile_list_keypoint_patch_change_kernel(tc, tab_words, tab_scales, offs, w1, 
                     start=True,
                     stop=True,
                 )
+            final = first + width == S
             for n in range(N_TILES):
                 nc.scalar.activation(out=result[:, n, cols], in_=ys[n], func=ACT.Tanh, bias=bias[:, n : n + 1])
-            nc.sync.dma_start(out=out_view[:, :, cols], in_=result[:, :, cols])
+                if final:
+                    nc.sync.dma_start(out=out_view[:, n, cols], in_=result[:, n, cols])
+            if not final:
+                nc.sync.dma_start(out=out_view[:, :, cols], in_=result[:, :, cols])
 
-        free = [early[t][u] for t in range(2) for u in range(2)]
+        free = [early[t][u] for t in range(PAIR) for u in range(2)]
         half = CHUNK // 2
-        groups = [(c * CHUNK, CHUNK, [free[c][:, 0:CHUNK], free[c][:, CHUNK:BANK], late[c][:, 0, :]]) for c in range(CHUNKS - 1)]
-        last = (CHUNKS - 1) * CHUNK
-        tail_bank = late[CHUNKS - 1][:].rearrange("p t j -> p (t j)")
-        groups.append((last, half, [free[CHUNKS - 1][:, n * half : (n + 1) * half] for n in range(N_TILES)]))
-        groups.append((last + half, half, [tail_bank[:, n * half : (n + 1) * half] for n in range(N_TILES)]))
-        gather_g(3, 0 * CHUNK, CHUNK)
-        gather_g(3, 1 * CHUNK, CHUNK)
-        change(*groups[0][0:2])
-        change(*groups[1][0:2])
-        read_out(*groups[0])
-        gather_g(3, 2 * CHUNK, CHUNK)
-        change(*groups[2][0:2])
-        read_out(*groups[1])
-        gather_g(3, 3 * CHUNK, CHUNK)
-        change(*groups[3][0:2])
-        change(*groups[4][0:2])
-        read_out(*groups[2])
-        read_out(*groups[3])
-        read_out(*groups[4])
+        pieces = [(c * CHUNK, CHUNK) for c in range(CHUNKS - 1)] + [(S - CHUNK, half), (S - half, half)]
+        places = [[free[c][:, 0:CHUNK], free[c][:, CHUNK:BANK], late[c][:, 0, :]] for c in range(CHUNKS - 1)]
+        for bank in (free[-1][:], late[-1][:].rearrange("p t j -> p (t j)")):
+            places.append([bank[:, n * half : (n + 1) * half] for n in range(N_TILES)])
+
+        gather_g(LAST, 0, CHUNK)
+        gather_g(LAST, CHUNK, CHUNK)
+        change(*pieces[0])
+        change(*pieces[1])
+        read_out(*pieces[0], places[0])
+        gather_g(LAST, 2 * CHUNK, CHUNK)
+        change(*pieces[2])
+        read_out(*pieces[1], places[1])
+        gather_g(LAST, 3 * CHUNK, CHUNK)
+        change(*pieces[3])
+        change(*pieces[4])
+        for i in range(2, len(pieces)):
+            read_out(*pieces[i], places[i])

@@ -30,6 +30,8 @@ LAST = PACK - 1
 BANK = 512
 CHUNK = 256
 CHUNKS = S // CHUNK
+SLOT = {0: 0, 128: 256, 384: 0, 640: 256, 768: 384, 896: 0}
+VECTOR_SHARE = (64, 40, 64)
 
 
 def tile_list_keypoint_patch_change_kernel(tc, tab_words, tab_scales, offs, w1, gT, w4_words, w4_scales, b, out):
@@ -39,12 +41,11 @@ def tile_list_keypoint_patch_change_kernel(tc, tab_words, tab_scales, offs, w1, 
         psum = ctx.enter_context(tc.psum_pool(name="psum", bufs=1))
 
         offsets = keep.tile([P, S // GROUP], U16, name="offsets")
-        nc.sync.dma_start(offsets[:], offs)
 
         def picks(first, count):
             return offsets[:, first // GROUP : (first + count) // GROUP]
 
-        tab_sc = keep.tile([P, T // 4], I32, name="tab_sc", align_bytes=64)
+        tab_sc = keep.tile([P, T // 4], I32, name="tab_sc", tag="tab_sc", align_bytes=64)
         w4_sc = keep.tile([P, N // 4], I32, name="w4_sc", align_bytes=64)
         zero = keep.tile([P, 1], F32, name="zero")
         no_bias = keep.tile([P, 1], F32, name="no_bias")
@@ -59,90 +60,105 @@ def tile_list_keypoint_patch_change_kernel(tc, tab_words, tab_scales, offs, w1, 
         def load_tab(a):
             nc.sync.dma_start(out=tab[a][:], in_=tab_words[a].rearrange("p t i -> p (t i)").bitcast(I32))
 
+        def load_w(a):
+            nc.sync.dma_start(
+                out=w_raw[a][:], in_=w1[a * K_PASS : (a + 1) * K_PASS, :].rearrange("(p j) c -> p j c", j=PACK)
+            )
+
         load_tab(0)
+        nc.sync.dma_start(offsets[:], offs)
+        load_w(0)
         for q in range(QUADRANTS):
             nc.sync.dma_start(
                 out=tab_sc[32 * q : 32 * q + ROWS * PASSES, :],
                 in_=tab_scales[:, ROWS * q : ROWS * (q + 1), :].bitcast(I32),
             )
-        for a in range(PASSES):
-            nc.sync.dma_start(
-                out=w_raw[a][:], in_=w1[a * K_PASS : (a + 1) * K_PASS, :].rearrange("(p j) c -> p j c", j=PACK)
-            )
-            if a + 1 < PASSES:
-                load_tab(a + 1)
+        load_tab(1)
+        load_w(1)
+        load_w(2)
+        load_tab(2)
         g_planes = gT.rearrange("(p t) n -> t p n", t=PACK)
         g_all = [keep.tile([P, T], F32, name=f"g_all{t}") for t in range(PACK)]
         for t in range(PAIR):
             nc.sync.dma_start(out=g_all[t][:], in_=g_planes[t])
         w4_codes = keep.tile([P, 2 * N // 4], I32, name="w4_codes", align_bytes=64)
-        nc.sync.dma_start(out=w4_codes[:], in_=w4_words[0].bitcast(I32))
         for q in range(QUADRANTS):
             nc.sync.dma_start(
                 out=w4_sc[32 * q : 32 * q + ROWS, :], in_=w4_scales[0, ROWS * q : ROWS * (q + 1), :].bitcast(I32)
             )
         for t in range(PAIR, PACK):
             nc.sync.dma_start(out=g_all[t][:], in_=g_planes[t])
+        nc.sync.dma_start(out=w4_codes[:], in_=w4_words[0].bitcast(I32))
         bias = keep.tile([P, N_TILES], F32, name="bias")
         with nc.allow_non_contiguous_dma(reason="one bias value a partition"):
             nc.sync.dma_start(out=bias[:], in_=b.rearrange("(c p) -> p c", p=P))
 
+        halves = [slice(0, BANK), slice(BANK, S)]
         v_codes = keep.tile([P, PASSES, S], U32, name="v_codes", align_bytes=64)
 
-        def gather_words(a):
-            nc.vector.tensor_copy(out=v_codes[:, a, :], in_=tab[a][:].bitcast(U32).indirect(offsets[:]))
-
-        gather_words(0)
-        v_sc = keep.tile([P, S], U8, name="v_sc", align_bytes=64)
-        nc.vector.tensor_copy(out=v_sc[:], in_=tab_sc[:].bitcast(U8).indirect(offsets[:]))
+        def gather_words(a, first, count):
+            nc.vector.tensor_copy(
+                out=v_codes[:, a, first : first + count], in_=tab[a][:].bitcast(U32).indirect(picks(first, count))
+            )
 
         w_codes = keep.tile([P, PASSES, H], U32, name="w_codes", align_bytes=64)
-        w_sc = keep.tile([P, PASSES, H], U8, name="w_sc", align_bytes=64)
-        for a in range(PASSES):
+        w_sc = [None] + [keep.tile([P, H], U8, name=f"w_sc{a}", align_bytes=64) for a in range(1, PASSES)]
+
+        def quantise_w(a):
             w_bf = keep.tile([P, PACK, P, PACK], BF16, name=f"w_bf{a}", align_bytes=64)
             dst = w_bf[:].rearrange("p t m j -> p m j t")
             src = w_raw[a][:].rearrange("p j (m t) -> p m j t", t=PACK)
-            if a > 0:
-                nc.vector.tensor_copy(out=dst[:, 0 : P // 2], in_=src[:, 0 : P // 2])
-                nc.scalar.copy(out=dst[:, P // 2 : P], in_=src[:, P // 2 : P])
-            else:
-                nc.scalar.copy(out=dst, in_=src)
+            cut = VECTOR_SHARE[a]
+            nc.vector.tensor_copy(out=dst[:, 0:cut], in_=src[:, 0:cut])
+            nc.scalar.copy(out=dst[:, cut:P], in_=src[:, cut:P])
             nc.vector.quantize_mx(
                 out=w_codes[:, a, :].bitcast(FP8X4),
-                scales=w_sc[:, a, :],
+                scales=w_sc[a][:],
                 in_=w_bf[:].rearrange("p t m j -> p (t m j)"),
             )
 
-        def product(acc, t, a, cols):
+        v_sc = keep.tile([P, S], U8, name="v_sc", align_bytes=64)
+        banks = [[psum.tile([P, BANK], F32, name=f"bank{t}_{u}") for u in range(2)] for t in range(PACK)]
+
+        def product(t, u, a):
             nc.tensor.matmul_mx(
-                out=acc,
+                out=banks[t][u][:],
                 lhsT=w_codes[:, a, t * P : (t + 1) * P].bitcast(FP8X4),
-                lhsT_scale=w_sc[:, a, t * P : (t + 1) * P],
-                rhs=v_codes[:, a, cols].bitcast(FP8X4),
-                rhs_scale=v_sc[ROWS * a : P, cols],
+                lhsT_scale=w_sc[a][:, t * P : (t + 1) * P],
+                rhs=v_codes[:, a, halves[u]].bitcast(FP8X4),
+                rhs_scale=v_sc[ROWS * a : P, halves[u]],
                 start=(a == 0),
                 stop=(a == PASSES - 1),
             )
 
-        halves = [slice(0, BANK), slice(BANK, S)]
-        early = [[psum.tile([P, BANK], F32, name=f"early{t}_{u}") for u in range(2)] for t in range(PAIR)]
-        late = [psum.tile([P, PAIR, CHUNK], F32, name=f"late{c}") for c in range(CHUNKS)]
+        gather_words(0, 0, S)
+        nc.vector.tensor_copy(out=v_sc[:], in_=tab_sc[:].bitcast(U8).indirect(offsets[:]))
+        w_sc[0] = keep.tile([P, H], U8, name="w_sc0", tag="tab_sc", align_bytes=64)
+        quantise_w(0)
+        gather_words(1, 0, S)
+        quantise_w(1)
+        quantise_w(2)
+        for u in range(2):
+            gather_words(2, u * BANK, BANK)
         for a in range(PASSES):
-            if a > 0:
-                gather_words(a)
-            for u in range(2):
-                for t in range(PAIR):
-                    product(early[t][u][:], t, a, halves[u])
-        for c in range(CHUNKS):
-            for t in range(PAIR):
-                for a in range(PASSES):
-                    product(late[c][:, t, :], PAIR + t, a, slice(c * CHUNK, (c + 1) * CHUNK))
+            for t in range(PACK):
+                for u in range(2):
+                    product(t, u, a)
 
-        work = keep.tile([P, PACK * S + BANK], F32, name="work")
-        g_pick = work[:, 0 : PACK * S].rearrange("p (t j) -> p t j", t=PACK)
-        borrowed = work[:, PACK * S - BANK :].rearrange("p (t j) -> p t j", t=PAIR)
+        a_sb = keep.tile([P, PACK, S], F32, name="a_sb")
+        for t in range(PACK):
+            for u in range(2):
+                nc.scalar.copy(out=a_sb[:, t, halves[u]], in_=banks[t][u][:])
+
         diff_early = keep.tile([P, PAIR, S], F32, name="diff_early")
-        diff_late = keep.tile([P, PAIR, BANK], F32, name="diff_late")
+        late = keep.tile([P, 4 * S], F32, name="late")
+
+        def diff_pair(e, cols):
+            if e == 0:
+                return diff_early[:, :, cols]
+            step = S + SLOT[cols.start] - cols.start
+            return late[:, cols.start : cols.start + PAIR * step].rearrange("p (t j) -> p t j", t=PAIR)[:, :, 0 : cols.stop - cols.start]
+
         h_bf = keep.tile([P, S, PACK], BF16, name="h_bf", align_bytes=64)
         h_codes = keep.tile([P, S], U32, name="h_codes", align_bytes=64)
         h_sc = keep.tile([P, S], U8, name="h_sc", align_bytes=64)
@@ -151,41 +167,30 @@ def tile_list_keypoint_patch_change_kernel(tc, tab_words, tab_scales, offs, w1, 
         w4_bytes = w4_codes[:].bitcast(U8)
         w4_sc_bytes = w4_sc[:].bitcast(U8)
 
-        def gather_g(t, first, count):
-            nc.vector.tensor_copy(out=g_pick[:, t, first : first + count], in_=g_all[t][:].indirect(picks(first, count)))
+        def change(t, first, count):
+            cols = slice(first, first + count)
+            nc.vector.tensor_tensor(
+                out=diff_pair(t // PAIR, cols)[:, t % PAIR, :],
+                in0=g_all[t][:].indirect(picks(first, count)),
+                in1=a_sb[:, t, cols],
+                op=ALU.subtract,
+            )
 
-        def absolute(t0, cols, diff):
+        def absolute(e, cols):
             nc.scalar.activation(
-                out=h_bf[:, cols, t0 : t0 + PAIR].rearrange("p (c i) t -> p c t i", i=LINE),
-                in_=diff.rearrange("p t (c i) -> p c t i", i=LINE),
+                out=h_bf[:, cols, PAIR * e : PAIR * (e + 1)].rearrange("p (c i) t -> p c t i", i=LINE),
+                in_=diff_pair(e, cols).rearrange("p t (c i) -> p c t i", i=LINE),
                 func=ACT.Abs,
                 bias=no_bias[:],
             )
 
-        a_early = keep.tile([P, PAIR, S], F32, name="a_early")
-        for t in range(PAIR):
-            for u in range(2):
-                nc.scalar.copy(out=a_early[:, t, halves[u]], in_=early[t][u][:])
-        for t in range(PAIR):
-            for u in range(2):
-                gather_g(t, u * BANK, BANK)
-                nc.gpsimd.tensor_tensor(
-                    out=diff_early[:, t, halves[u]], in0=a_early[:, t, halves[u]], in1=g_pick[:, t, halves[u]], op=ALU.subtract
-                )
-        for u in range(2):
-            absolute(0, halves[u], diff_early[:, :, halves[u]])
-        gather_g(PAIR, 0, S)
-
-        def change(first, width):
-            cols = slice(first, first + width)
-            c, start = divmod(first, CHUNK)
-            diff = borrowed[:, :, cols] if first < BANK else diff_late[:, :, first - BANK : first - BANK + width]
-            nc.vector.tensor_tensor(
-                out=diff, in0=late[c][:, :, start : start + width], in1=g_pick[:, PAIR:PACK, cols], op=ALU.subtract
+        def absolute_on_vector(cols):
+            diff = diff_pair(1, cols).rearrange("p t j -> p j t")
+            nc.vector.scalar_tensor_tensor(
+                out=h_bf[:, cols, PAIR:PACK], in0=diff, scalar=-1.0, in1=diff, op0=ALU.mult, op1=ALU.max
             )
-            absolute(PAIR, cols, diff)
 
-        def read_out(first, width, ys):
+        def read_out(first, width, ys, final):
             cols = slice(first, first + width)
             nc.vector.quantize_mx(
                 out=h_codes[:, cols].bitcast(FP8X4),
@@ -202,7 +207,6 @@ def tile_list_keypoint_patch_change_kernel(tc, tab_words, tab_scales, offs, w1, 
                     start=True,
                     stop=True,
                 )
-            final = first + width == S
             for n in range(N_TILES):
                 nc.scalar.activation(out=result[:, n, cols], in_=ys[n], func=ACT.Tanh, bias=bias[:, n : n + 1])
                 if final:
@@ -210,23 +214,29 @@ def tile_list_keypoint_patch_change_kernel(tc, tab_words, tab_scales, offs, w1, 
             if not final:
                 nc.sync.dma_start(out=out_view[:, :, cols], in_=result[:, :, cols])
 
-        free = [early[t][u] for t in range(PAIR) for u in range(2)]
-        half = CHUNK // 2
-        pieces = [(c * CHUNK, CHUNK) for c in range(CHUNKS - 1)] + [(S - CHUNK, half), (S - half, half)]
-        places = [[free[c][:, 0:CHUNK], free[c][:, CHUNK:BANK], late[c][:, 0, :]] for c in range(CHUNKS - 1)]
-        for bank in (free[-1][:], late[-1][:].rearrange("p t j -> p (t j)")):
-            places.append([bank[:, n * half : (n + 1) * half] for n in range(N_TILES)])
+        for t in range(PAIR):
+            for u in range(2):
+                change(t, u * BANK, BANK)
+                if t == 1:
+                    absolute(0, halves[u])
+        nc.vector.tensor_tensor(out=late[:, 0:S], in0=g_all[PAIR][:].indirect(offsets[:]), in1=a_sb[:, PAIR, :], op=ALU.subtract)
 
-        gather_g(LAST, 0, CHUNK)
-        gather_g(LAST, CHUNK, CHUNK)
-        change(*pieces[0])
-        change(*pieces[1])
-        read_out(*pieces[0], places[0])
-        gather_g(LAST, 2 * CHUNK, CHUNK)
-        change(*pieces[2])
-        read_out(*pieces[1], places[1])
-        gather_g(LAST, 3 * CHUNK, CHUNK)
-        change(*pieces[3])
-        change(*pieces[4])
-        for i in range(2, len(pieces)):
-            read_out(*pieces[i], places[i])
+        free = [banks[t][u] for t in range(PACK) for u in range(2)]
+        change(LAST, 0, 128)
+        absolute(1, slice(0, 128))
+        change(LAST, 128, 256)
+        absolute(1, slice(128, 384))
+        read_out(0, 128, [free[0][:, n * 128 : (n + 1) * 128] for n in range(N_TILES)], False)
+        change(LAST, 384, 256)
+        absolute(1, slice(384, 640))
+        read_out(128, 256, [free[1][:, 0:256], free[1][:, 256:512], free[2][:, 0:256]], False)
+        change(LAST, 640, 128)
+        change(LAST, 768, 128)
+        absolute(1, slice(768, 896))
+        absolute_on_vector(slice(640, 768))
+        read_out(640, 128, [free[5][:, n * 128 : (n + 1) * 128] for n in range(N_TILES)], False)
+        read_out(384, 256, [free[3][:, 0:256], free[3][:, 256:512], free[4][:, 0:256]], True)
+        change(LAST, 896, 128)
+        absolute_on_vector(slice(896, 1024))
+        read_out(896, 128, [free[7][:, n * 128 : (n + 1) * 128] for n in range(N_TILES)], False)
+        read_out(768, 128, [free[6][:, n * 128 : (n + 1) * 128] for n in range(N_TILES)], True)

@@ -30,8 +30,11 @@ LAST = PACK - 1
 BANK = 512
 CHUNK = 256
 CHUNKS = S // CHUNK
-SLOT = {0: 0, 128: 256, 384: 0, 640: 256, 768: 384, 896: 0}
-VECTOR_SHARE = (64, 40, 64)
+PIECES = [(0, 128), (128, 256), (384, 256), (640, 256), (896, 128)]
+H_AT = {0:1536,128:1920,384:2432,640:2944,896:3456}
+CODES_AT = {}
+SLOT = {0: 0, 128: 128, 384: 384, 640: 640, 896: 1408}
+VECTOR_SHARE = (64, 24, 64)
 
 
 def tile_list_keypoint_patch_change_kernel(tc, tab_words, tab_scales, offs, w1, gT, w4_words, w4_scales, b, out):
@@ -140,18 +143,17 @@ def tile_list_keypoint_patch_change_kernel(tc, tab_words, tab_scales, offs, w1, 
         quantise_w(2)
         for u in range(2):
             gather_words(2, u * BANK, BANK)
+        order = [(PAIR * e + t, u) for e in range(PACK // PAIR) for u in range(2) for t in range(PAIR)]
         for a in range(PASSES):
-            for t in range(PACK):
-                for u in range(2):
-                    product(t, u, a)
+            for t, u in order:
+                product(t, u, a)
 
         a_sb = keep.tile([P, PACK, S], F32, name="a_sb")
-        for t in range(PACK):
-            for u in range(2):
-                nc.scalar.copy(out=a_sb[:, t, halves[u]], in_=banks[t][u][:])
+        for t, u in order:
+            nc.scalar.copy(out=a_sb[:, t, halves[u]], in_=banks[t][u][:])
 
         diff_early = keep.tile([P, PAIR, S], F32, name="diff_early")
-        late = keep.tile([P, 4 * S], F32, name="late")
+        late = keep.tile([P, 4096], F32, name="late", align_bytes=64)
 
         def diff_pair(e, cols):
             if e == 0:
@@ -159,8 +161,10 @@ def tile_list_keypoint_patch_change_kernel(tc, tab_words, tab_scales, offs, w1, 
             step = S + SLOT[cols.start] - cols.start
             return late[:, cols.start : cols.start + PAIR * step].rearrange("p (t j) -> p t j", t=PAIR)[:, :, 0 : cols.stop - cols.start]
 
-        h_bf = keep.tile([P, S, PACK], BF16, name="h_bf", align_bytes=64)
-        h_codes = keep.tile([P, S], U32, name="h_codes", align_bytes=64)
+        h_bf = {
+            first: late[:, H_AT[first] : H_AT[first] + PAIR * width].bitcast(BF16).rearrange("p (j t) -> p j t", t=PACK)
+            for first, width in PIECES
+        }
         h_sc = keep.tile([P, S], U8, name="h_sc", align_bytes=64)
         result = keep.tile([P, N_TILES, S], F32, name="result")
         out_view = out.rearrange("(c p) j -> p c j", p=P)
@@ -178,7 +182,7 @@ def tile_list_keypoint_patch_change_kernel(tc, tab_words, tab_scales, offs, w1, 
 
         def absolute(e, cols):
             nc.scalar.activation(
-                out=h_bf[:, cols, PAIR * e : PAIR * (e + 1)].rearrange("p (c i) t -> p c t i", i=LINE),
+                out=h_bf[cols.start][:, :, PAIR * e : PAIR * (e + 1)].rearrange("p (c i) t -> p c t i", i=LINE),
                 in_=diff_pair(e, cols).rearrange("p t (c i) -> p c t i", i=LINE),
                 func=ACT.Abs,
                 bias=no_bias[:],
@@ -187,56 +191,70 @@ def tile_list_keypoint_patch_change_kernel(tc, tab_words, tab_scales, offs, w1, 
         def absolute_on_vector(cols):
             diff = diff_pair(1, cols).rearrange("p t j -> p j t")
             nc.vector.scalar_tensor_tensor(
-                out=h_bf[:, cols, PAIR:PACK], in0=diff, scalar=-1.0, in1=diff, op0=ALU.mult, op1=ALU.max
+                out=h_bf[cols.start][:, :, PAIR:PACK], in0=diff, scalar=-1.0, in1=diff, op0=ALU.mult, op1=ALU.max
             )
 
-        def read_out(first, width, ys, final):
+        def score(first, width, ys):
             cols = slice(first, first + width)
+            if first in CODES_AT:
+                h_codes = late[:, CODES_AT[first] : CODES_AT[first] + width].bitcast(U32)
+            else:
+                h_codes = keep.tile([P, width], U32, name=f"h_codes{first}", align_bytes=64)[:]
             nc.vector.quantize_mx(
-                out=h_codes[:, cols].bitcast(FP8X4),
+                out=h_codes.bitcast(FP8X4),
                 scales=h_sc[:, cols],
-                in_=h_bf[:, cols, :].rearrange("p j t -> p (j t)"),
+                in_=h_bf[first].rearrange("p j t -> p (j t)"),
             )
             for n in range(N_TILES):
                 nc.tensor.matmul_mx(
                     out=ys[n],
                     lhsT=w4_bytes[:, 2 * P * n : 2 * P * (n + 1)].bitcast(FP4X4),
                     lhsT_scale=w4_sc_bytes[:, P * n : P * (n + 1)],
-                    rhs=h_codes[:, cols].bitcast(FP8X4),
+                    rhs=h_codes.bitcast(FP8X4),
                     rhs_scale=h_sc[:, cols],
                     start=True,
                     stop=True,
                 )
+
+        def finish(first, width, ys, final):
+            cols = slice(first, first + width)
+            stored = 0
             for n in range(N_TILES):
                 nc.scalar.activation(out=result[:, n, cols], in_=ys[n], func=ACT.Tanh, bias=bias[:, n : n + 1])
-                if final:
-                    nc.sync.dma_start(out=out_view[:, n, cols], in_=result[:, n, cols])
-            if not final:
-                nc.sync.dma_start(out=out_view[:, :, cols], in_=result[:, :, cols])
+                if n in final:
+                    nc.sync.dma_start(out=out_view[:, stored : n + 1, cols], in_=result[:, stored : n + 1, cols])
+                    stored = n + 1
 
         for t in range(PAIR):
             for u in range(2):
                 change(t, u * BANK, BANK)
-                if t == 1:
-                    absolute(0, halves[u])
+        for first, width in PIECES:
+            absolute(0, slice(first, first + width))
         nc.vector.tensor_tensor(out=late[:, 0:S], in0=g_all[PAIR][:].indirect(offsets[:]), in1=a_sb[:, PAIR, :], op=ALU.subtract)
 
         free = [banks[t][u] for t in range(PACK) for u in range(2)]
+        ys_A = [free[0][:, n * 128 : (n + 1) * 128] for n in range(N_TILES)]
+        ys_B = [free[1][:, 0:256], free[1][:, 256:512], free[2][:, 0:256]]
+        ys_C = [free[3][:, 0:256], free[3][:, 256:512], free[4][:, 0:256]]
+        ys_D = [free[5][:, 0:256], free[5][:, 256:512], free[6][:, 0:256]]
+        ys_F = [free[7][:, n * 128 : (n + 1) * 128] for n in range(N_TILES)]
         change(LAST, 0, 128)
         absolute(1, slice(0, 128))
         change(LAST, 128, 256)
         absolute(1, slice(128, 384))
-        read_out(0, 128, [free[0][:, n * 128 : (n + 1) * 128] for n in range(N_TILES)], False)
+        score(0, 128, ys_A)
         change(LAST, 384, 256)
         absolute(1, slice(384, 640))
-        read_out(128, 256, [free[1][:, 0:256], free[1][:, 256:512], free[2][:, 0:256]], False)
-        change(LAST, 640, 128)
-        change(LAST, 768, 128)
-        absolute(1, slice(768, 896))
-        absolute_on_vector(slice(640, 768))
-        read_out(640, 128, [free[5][:, n * 128 : (n + 1) * 128] for n in range(N_TILES)], False)
-        read_out(384, 256, [free[3][:, 0:256], free[3][:, 256:512], free[4][:, 0:256]], True)
+        finish(0, 128, ys_A, (2,))
+        change(LAST, 640, 256)
+        score(128, 256, ys_B)
+        finish(128, 256, ys_B, (0, 1, 2))
+        score(384, 256, ys_C)
+        absolute_on_vector(slice(640, 896))
+        finish(384, 256, ys_C, (0, 1, 2))
         change(LAST, 896, 128)
+        score(640, 256, ys_D)
         absolute_on_vector(slice(896, 1024))
-        read_out(896, 128, [free[7][:, n * 128 : (n + 1) * 128] for n in range(N_TILES)], False)
-        read_out(768, 128, [free[6][:, n * 128 : (n + 1) * 128] for n in range(N_TILES)], True)
+        finish(640, 256, ys_D, (0, 1, 2))
+        score(896, 128, ys_F)
+        finish(896, 128, ys_F, (1, 2))

@@ -1,6 +1,7 @@
 from contextlib import ExitStack
 
 import concourse.mybir as mybir
+from concourse.masks import make_identity
 
 K, T, S, H, N = 1536, 2048, 1024, 512, 384
 FLOPS = 2 * K * H * S + 2 * H * N * S
@@ -28,12 +29,8 @@ LINE = 4
 PAIR = 2
 LAST = PACK - 1
 BANK = 512
-CHUNK = 256
-CHUNKS = S // CHUNK
-PIECES = [(0, 128), (128, 256), (384, 256), (640, 256), (896, 128)]
-H_AT = {0:1536,128:1920,384:2432,640:2944,896:3456}
-CODES_AT = {}
-SLOT = {0: 0, 128: 128, 384: 384, 640: 640, 896: 1408}
+WIDE, NARROW = 256, 128
+WIDTHS = (WIDE, WIDE, WIDE, NARROW, NARROW)
 VECTOR_SHARE = (64, 24, 64)
 
 
@@ -45,14 +42,18 @@ def tile_list_keypoint_patch_change_kernel(tc, tab_words, tab_scales, offs, w1, 
 
         offsets = keep.tile([P, S // GROUP], U16, name="offsets")
 
-        def picks(first, count):
-            return offsets[:, first // GROUP : (first + count) // GROUP]
+        def picks(cols):
+            return offsets[:, cols.start // GROUP : cols.stop // GROUP]
 
         tab_sc = keep.tile([P, T // 4], I32, name="tab_sc", tag="tab_sc", align_bytes=64)
         w4_sc = keep.tile([P, N // 4], I32, name="w4_sc", align_bytes=64)
         zero = keep.tile([P, 1], F32, name="zero")
         no_bias = keep.tile([P, 1], F32, name="no_bias")
+        b_row = keep.tile([P, N], F32, name="b_row")
+        identity = keep.tile([P, P], F32, name="identity")
         nc.gpsimd.memset(tab_sc[:], 0)
+        make_identity(nc, identity[:])
+        nc.vector.memset(b_row[:], 0.0)
         nc.vector.memset(w4_sc[:], 0)
         nc.vector.memset(zero[:], 0.0)
         nc.scalar.activation(out=no_bias[:], in_=zero[:], func=ACT.Tanh)
@@ -70,6 +71,7 @@ def tile_list_keypoint_patch_change_kernel(tc, tab_words, tab_scales, offs, w1, 
 
         load_tab(0)
         nc.sync.dma_start(offsets[:], offs)
+        nc.sync.dma_start(out=b_row[0:1, :], in_=b.rearrange("(o n) -> o n", o=1))
         load_w(0)
         for q in range(QUADRANTS):
             nc.sync.dma_start(
@@ -85,27 +87,22 @@ def tile_list_keypoint_patch_change_kernel(tc, tab_words, tab_scales, offs, w1, 
         for t in range(PAIR):
             nc.sync.dma_start(out=g_all[t][:], in_=g_planes[t])
         w4_codes = keep.tile([P, 2 * N // 4], I32, name="w4_codes", align_bytes=64)
+        nc.sync.dma_start(out=w4_codes[:], in_=w4_words[0].bitcast(I32))
         for q in range(QUADRANTS):
             nc.sync.dma_start(
                 out=w4_sc[32 * q : 32 * q + ROWS, :], in_=w4_scales[0, ROWS * q : ROWS * (q + 1), :].bitcast(I32)
             )
         for t in range(PAIR, PACK):
             nc.sync.dma_start(out=g_all[t][:], in_=g_planes[t])
-        nc.sync.dma_start(out=w4_codes[:], in_=w4_words[0].bitcast(I32))
-        bias = keep.tile([P, N_TILES], F32, name="bias")
-        with nc.allow_non_contiguous_dma(reason="one bias value a partition"):
-            nc.sync.dma_start(out=bias[:], in_=b.rearrange("(c p) -> p c", p=P))
 
+        everything = slice(0, S)
         halves = [slice(0, BANK), slice(BANK, S)]
         v_codes = keep.tile([P, PASSES, S], U32, name="v_codes", align_bytes=64)
-
-        def gather_words(a, first, count):
-            nc.vector.tensor_copy(
-                out=v_codes[:, a, first : first + count], in_=tab[a][:].bitcast(U32).indirect(picks(first, count))
-            )
-
         w_codes = keep.tile([P, PASSES, H], U32, name="w_codes", align_bytes=64)
-        w_sc = [None] + [keep.tile([P, H], U8, name=f"w_sc{a}", align_bytes=64) for a in range(1, PASSES)]
+        w_sc = {a: keep.tile([P, H], U8, name=f"w_sc{a}", align_bytes=64) for a in range(1, PASSES)}
+
+        def gather_words(a, cols):
+            nc.vector.tensor_copy(out=v_codes[:, a, cols], in_=tab[a][:].bitcast(U32).indirect(picks(cols)))
 
         def quantise_w(a):
             w_bf = keep.tile([P, PACK, P, PACK], BF16, name=f"w_bf{a}", align_bytes=64)
@@ -121,140 +118,152 @@ def tile_list_keypoint_patch_change_kernel(tc, tab_words, tab_scales, offs, w1, 
             )
 
         v_sc = keep.tile([P, S], U8, name="v_sc", align_bytes=64)
-        banks = [[psum.tile([P, BANK], F32, name=f"bank{t}_{u}") for u in range(2)] for t in range(PACK)]
+        banks = [[psum.tile([P, BANK], F32, name=f"bank{t}_{u}") for u in range(len(halves))] for t in range(PACK)]
 
-        def product(t, u, a):
-            nc.tensor.matmul_mx(
-                out=banks[t][u][:],
-                lhsT=w_codes[:, a, t * P : (t + 1) * P].bitcast(FP8X4),
-                lhsT_scale=w_sc[a][:, t * P : (t + 1) * P],
-                rhs=v_codes[:, a, halves[u]].bitcast(FP8X4),
-                rhs_scale=v_sc[ROWS * a : P, halves[u]],
-                start=(a == 0),
-                stop=(a == PASSES - 1),
-            )
+        bias = keep.tile([P, N_TILES], F32, name="bias")
+        for n in range(N_TILES):
+            nc.tensor.transpose(banks[LAST][1][:, n * P : (n + 1) * P], b_row[:, n * P : (n + 1) * P], identity[:])
+        nc.scalar.copy(out=bias[:], in_=banks[LAST][1][:, 0:N:P])
 
-        gather_words(0, 0, S)
+        gather_words(0, everything)
         nc.vector.tensor_copy(out=v_sc[:], in_=tab_sc[:].bitcast(U8).indirect(offsets[:]))
         w_sc[0] = keep.tile([P, H], U8, name="w_sc0", tag="tab_sc", align_bytes=64)
         quantise_w(0)
-        gather_words(1, 0, S)
+        gather_words(1, everything)
         quantise_w(1)
         quantise_w(2)
-        for u in range(2):
-            gather_words(2, u * BANK, BANK)
-        order = [(PAIR * e + t, u) for e in range(PACK // PAIR) for u in range(2) for t in range(PAIR)]
+        for cols in halves:
+            gather_words(2, cols)
+
+        order = [(PAIR * e + t, u) for e in range(PACK // PAIR) for u in range(len(halves)) for t in range(PAIR)]
         for a in range(PASSES):
             for t, u in order:
-                product(t, u, a)
+                nc.tensor.matmul_mx(
+                    out=banks[t][u][:],
+                    lhsT=w_codes[:, a, t * P : (t + 1) * P].bitcast(FP8X4),
+                    lhsT_scale=w_sc[a][:, t * P : (t + 1) * P],
+                    rhs=v_codes[:, a, halves[u]].bitcast(FP8X4),
+                    rhs_scale=v_sc[ROWS * a : P, halves[u]],
+                    start=(a == 0),
+                    stop=(a == PASSES - 1),
+                )
 
+        run = [WIDE] + [BANK] * LAST
         a_sb = keep.tile([P, PACK, S], F32, name="a_sb")
         for t, u in order:
-            nc.scalar.copy(out=a_sb[:, t, halves[u]], in_=banks[t][u][:])
+            for first in range(0, BANK, run[t]):
+                nc.scalar.copy(
+                    out=a_sb[:, t, u * BANK + first : u * BANK + first + run[t]],
+                    in_=banks[t][u][:, first : first + run[t]],
+                )
 
+        pieces = [slice(sum(WIDTHS[:i]), sum(WIDTHS[: i + 1])) for i in range(len(WIDTHS))]
+        wide_end = pieces[2].stop
+        h_first = PAIR * wide_end
+        diff_at = [(cols.start, wide_end + cols.start) for cols in pieces[:3]]
+        diff_at.extend((h_first + k * NARROW, h_first + WIDE + k * NARROW) for k in range(2))
+        late = keep.tile([P, h_first + PAIR * WIDE + NARROW], F32, name="late", align_bytes=64)
         diff_early = keep.tile([P, PAIR, S], F32, name="diff_early")
-        late = keep.tile([P, 4096], F32, name="late", align_bytes=64)
-
-        def diff_pair(e, cols):
-            if e == 0:
-                return diff_early[:, :, cols]
-            step = S + SLOT[cols.start] - cols.start
-            return late[:, cols.start : cols.start + PAIR * step].rearrange("p (t j) -> p t j", t=PAIR)[:, :, 0 : cols.stop - cols.start]
-
-        h_bf = {
-            first: late[:, H_AT[first] : H_AT[first] + PAIR * width].bitcast(BF16).rearrange("p (j t) -> p j t", t=PACK)
-            for first, width in PIECES
-        }
+        h_bf = [late[:, h_first : h_first + PAIR * WIDE].bitcast(BF16).rearrange("p (j t) -> p j t", t=PACK)]
+        for i in range(1, len(WIDTHS)):
+            h_bf.append(keep.tile([P, WIDTHS[i], PACK], BF16, name=f"h_bf{i}", align_bytes=64)[:])
         h_sc = keep.tile([P, S], U8, name="h_sc", align_bytes=64)
         result = keep.tile([P, N_TILES, S], F32, name="result")
         out_view = out.rearrange("(c p) j -> p c j", p=P)
         w4_bytes = w4_codes[:].bitcast(U8)
         w4_sc_bytes = w4_sc[:].bitcast(U8)
 
-        def change(t, first, count):
-            cols = slice(first, first + count)
+        def subtract(t, cols, diff):
             nc.vector.tensor_tensor(
-                out=diff_pair(t // PAIR, cols)[:, t % PAIR, :],
-                in0=g_all[t][:].indirect(picks(first, count)),
+                out=diff,
+                in0=g_all[t][:].indirect(picks(cols)),
                 in1=a_sb[:, t, cols],
                 op=ALU.subtract,
             )
 
-        def absolute(e, cols):
+        def late_pair(i):
+            first, second = diff_at[i]
+            apart = second - first
+            return late[:, first : first + PAIR * apart].rearrange("p (t j) -> p t j", t=PAIR)[:, :, 0 : WIDTHS[i]]
+
+        def abs_on_scalar(i, first_plane, diff):
             nc.scalar.activation(
-                out=h_bf[cols.start][:, :, PAIR * e : PAIR * (e + 1)].rearrange("p (c i) t -> p c t i", i=LINE),
-                in_=diff_pair(e, cols).rearrange("p t (c i) -> p c t i", i=LINE),
+                out=h_bf[i][:, :, first_plane : first_plane + PAIR].rearrange("p (c i) t -> p c t i", i=LINE),
+                in_=diff.rearrange("p t (c i) -> p c t i", i=LINE),
                 func=ACT.Abs,
                 bias=no_bias[:],
             )
 
-        def absolute_on_vector(cols):
-            diff = diff_pair(1, cols).rearrange("p t j -> p j t")
+        def abs_on_vector(i):
+            diff = late_pair(i).rearrange("p t j -> p j t")
             nc.vector.scalar_tensor_tensor(
-                out=h_bf[cols.start][:, :, PAIR:PACK], in0=diff, scalar=-1.0, in1=diff, op0=ALU.mult, op1=ALU.max
+                out=h_bf[i][:, :, PAIR:PACK], in0=diff, scalar=-1.0, in1=diff, op0=ALU.mult, op1=ALU.max
             )
 
-        def score(first, width, ys):
-            cols = slice(first, first + width)
-            if first in CODES_AT:
-                h_codes = late[:, CODES_AT[first] : CODES_AT[first] + width].bitcast(U32)
-            else:
-                h_codes = keep.tile([P, width], U32, name=f"h_codes{first}", align_bytes=64)[:]
+        def subtract_late(t, i, count=1):
+            cols = slice(pieces[i].start, pieces[i + count - 1].stop)
+            at = diff_at[i][t - PAIR]
+            subtract(t, cols, late[:, at : at + cols.stop - cols.start])
+
+        free = [banks[t][u] for t, u in order]
+        places = []
+        for width in WIDTHS:
+            per_bank = BANK // width
+            mine = [free.pop(0) for k in range(0, N_TILES, per_bank)]
+            places.append(
+                [mine[n // per_bank][:, n % per_bank * width : (n % per_bank + 1) * width] for n in range(N_TILES)]
+            )
+
+        def score(i):
+            h_codes = keep.tile([P, WIDTHS[i]], U32, name=f"h_codes{i}", align_bytes=64)
             nc.vector.quantize_mx(
-                out=h_codes.bitcast(FP8X4),
-                scales=h_sc[:, cols],
-                in_=h_bf[first].rearrange("p j t -> p (j t)"),
+                out=h_codes[:].bitcast(FP8X4),
+                scales=h_sc[:, pieces[i]],
+                in_=h_bf[i].rearrange("p j t -> p (j t)"),
             )
             for n in range(N_TILES):
                 nc.tensor.matmul_mx(
-                    out=ys[n],
+                    out=places[i][n],
                     lhsT=w4_bytes[:, 2 * P * n : 2 * P * (n + 1)].bitcast(FP4X4),
                     lhsT_scale=w4_sc_bytes[:, P * n : P * (n + 1)],
-                    rhs=h_codes.bitcast(FP8X4),
-                    rhs_scale=h_sc[:, cols],
+                    rhs=h_codes[:].bitcast(FP8X4),
+                    rhs_scale=h_sc[:, pieces[i]],
                     start=True,
                     stop=True,
                 )
 
-        def finish(first, width, ys, final):
-            cols = slice(first, first + width)
+        def finish(i, store_after):
+            cols = pieces[i]
             stored = 0
             for n in range(N_TILES):
-                nc.scalar.activation(out=result[:, n, cols], in_=ys[n], func=ACT.Tanh, bias=bias[:, n : n + 1])
-                if n in final:
+                nc.scalar.activation(out=result[:, n, cols], in_=places[i][n], func=ACT.Tanh, bias=bias[:, n : n + 1])
+                if n in store_after:
                     nc.sync.dma_start(out=out_view[:, stored : n + 1, cols], in_=result[:, stored : n + 1, cols])
                     stored = n + 1
 
         for t in range(PAIR):
-            for u in range(2):
-                change(t, u * BANK, BANK)
-        for first, width in PIECES:
-            absolute(0, slice(first, first + width))
-        nc.vector.tensor_tensor(out=late[:, 0:S], in0=g_all[PAIR][:].indirect(offsets[:]), in1=a_sb[:, PAIR, :], op=ALU.subtract)
+            for first in range(0, S, run[t]):
+                cols = slice(first, first + run[t])
+                subtract(t, cols, diff_early[:, t, cols])
+        for i, cols in enumerate(pieces):
+            abs_on_scalar(i, 0, diff_early[:, :, cols])
+        subtract_late(PAIR, 0, count=3)
 
-        free = [banks[t][u] for t in range(PACK) for u in range(2)]
-        ys_A = [free[0][:, n * 128 : (n + 1) * 128] for n in range(N_TILES)]
-        ys_B = [free[1][:, 0:256], free[1][:, 256:512], free[2][:, 0:256]]
-        ys_C = [free[3][:, 0:256], free[3][:, 256:512], free[4][:, 0:256]]
-        ys_D = [free[5][:, 0:256], free[5][:, 256:512], free[6][:, 0:256]]
-        ys_F = [free[7][:, n * 128 : (n + 1) * 128] for n in range(N_TILES)]
-        change(LAST, 0, 128)
-        absolute(1, slice(0, 128))
-        change(LAST, 128, 256)
-        absolute(1, slice(128, 384))
-        score(0, 128, ys_A)
-        change(LAST, 384, 256)
-        absolute(1, slice(384, 640))
-        finish(0, 128, ys_A, (2,))
-        change(LAST, 640, 256)
-        score(128, 256, ys_B)
-        finish(128, 256, ys_B, (0, 1, 2))
-        score(384, 256, ys_C)
-        absolute_on_vector(slice(640, 896))
-        finish(384, 256, ys_C, (0, 1, 2))
-        change(LAST, 896, 128)
-        score(640, 256, ys_D)
-        absolute_on_vector(slice(896, 1024))
-        finish(640, 256, ys_D, (0, 1, 2))
-        score(896, 128, ys_F)
-        finish(896, 128, ys_F, (1, 2))
+        whole, two_parts, by_tile = (2,), (1, 2), (0, 1, 2)
+        for i in range(3):
+            subtract_late(LAST, i)
+            abs_on_scalar(i, PAIR, late_pair(i))
+        score(0)
+        subtract_late(PAIR, 3, count=2)
+        score(1)
+        finish(0, two_parts)
+        finish(1, by_tile)
+        subtract_late(LAST, 3, count=2)
+        score(2)
+        finish(2, by_tile)
+        abs_on_vector(3)
+        abs_on_vector(4)
+        score(3)
+        score(4)
+        finish(3, whole)
+        finish(4, two_parts)

@@ -208,11 +208,12 @@ def tile_list_keypoint_patch_change_kernel(tc, tab_words, tab_scales, offs, w1, 
         free = [banks[t][u] for t, u in order]
         places = []
         for width in WIDTHS:
-            per_bank = BANK // width
-            mine = [free.pop(0) for k in range(0, N_TILES, per_bank)]
-            places.append(
-                [mine[n // per_bank][:, n % per_bank * width : (n % per_bank + 1) * width] for n in range(N_TILES)]
-            )
+            if width == WIDE:
+                alone, shared = free.pop(0), free.pop(0)
+                places.append([alone[:, 0:width], shared[:, 0:width], shared[:, width : 2 * width]])
+            else:
+                mine = free.pop(0)
+                places.append([mine[:, n * width : (n + 1) * width] for n in range(N_TILES)])
 
         def score(i):
             h_codes = keep.tile([P, WIDTHS[i]], U32, name=f"h_codes{i}", align_bytes=64)

@@ -84,7 +84,7 @@ def tile_list_keypoint_patch_change_kernel(tc, tab_words, tab_scales, offs, w1, 
         load_tab(2)
         g_planes = gT.rearrange("(p t) n -> t p n", t=PACK)
         g_all = [keep.tile([P, T], F32, name=f"g_all{t}") for t in range(PACK)]
-        for t in range(PAIR):
+        for t in range(PACK):
             nc.sync.dma_start(out=g_all[t][:], in_=g_planes[t])
         w4_codes = keep.tile([P, 2 * N // 4], I32, name="w4_codes", align_bytes=64)
         nc.sync.dma_start(out=w4_codes[:], in_=w4_words[0].bitcast(I32))
@@ -92,8 +92,6 @@ def tile_list_keypoint_patch_change_kernel(tc, tab_words, tab_scales, offs, w1, 
             nc.sync.dma_start(
                 out=w4_sc[32 * q : 32 * q + ROWS, :], in_=w4_scales[0, ROWS * q : ROWS * (q + 1), :].bitcast(I32)
             )
-        for t in range(PAIR, PACK):
-            nc.sync.dma_start(out=g_all[t][:], in_=g_planes[t])
 
         everything = slice(0, S)
         halves = [slice(0, BANK), slice(BANK, S)]

@@ -159,8 +159,8 @@ def tile_list_keypoint_patch_change_kernel(tc, tab_words, tab_scales, offs, w1, 
         wide_end = pieces[2].stop
         h_first = PAIR * wide_end
         diff_at = [(cols.start, wide_end + cols.start) for cols in pieces[:3]]
-        diff_at.extend((h_first + k * NARROW, h_first + WIDE + k * NARROW) for k in range(2))
-        late = keep.tile([P, h_first + PAIR * WIDE + NARROW], F32, name="late", align_bytes=64)
+        diff_at.extend((k * NARROW, h_first + k * NARROW) for k in range(2))
+        late = keep.tile([P, PAIR * h_first + NARROW], F32, name="late", align_bytes=64)
         diff_early = keep.tile([P, PAIR, S], F32, name="diff_early")
         h_bf = [late[:, h_first : h_first + PAIR * WIDE].bitcast(BF16).rearrange("p (j t) -> p j t", t=PACK)]
         for i in range(1, len(WIDTHS)):

from contextlib import ExitStack

import concourse.mybir as mybir
from concourse.masks import make_identity

K, T, S, H, N = 1536, 2048, 1024, 512, 384
FLOPS = 2 * K * H * S + 2 * H * N * S

F32 = mybir.dt.float32
BF16 = mybir.dt.bfloat16
I32 = mybir.dt.int32
U32 = mybir.dt.uint32
U16 = mybir.dt.uint16
U8 = mybir.dt.uint8
FP8X4 = mybir.dt.float8_e4m3fn_x4
FP4X4 = mybir.dt.float4_e2m1fn_x4
ACT = mybir.ActivationFunctionType
ALU = mybir.AluOpType

P = 128
PACK = 4
K_PASS = P * PACK
PASSES = K // K_PASS
N_TILES = N // P
QUADRANTS = 4
ROWS = 4
GROUP = 16
LINE = 4
PAIR = 2
LAST = PACK - 1
BANK = 512
WIDE, NARROW = 256, 128
WIDTHS = (WIDE, WIDE, WIDE, NARROW, NARROW)
VECTOR_SHARE = (64, 24, 64)


def tile_list_keypoint_patch_change_kernel(tc, tab_words, tab_scales, offs, w1, gT, w4_words, w4_scales, b, out):
    nc = tc.nc
    with ExitStack() as ctx:
        keep = ctx.enter_context(tc.tile_pool(name="keep", bufs=1))
        psum = ctx.enter_context(tc.psum_pool(name="psum", bufs=1))

        offsets = keep.tile([P, S // GROUP], U16, name="offsets")

        def picks(cols):
            return offsets[:, cols.start // GROUP : cols.stop // GROUP]

        tab_sc = keep.tile([P, T // 4], I32, name="tab_sc", tag="tab_sc", align_bytes=64)
        w4_sc = keep.tile([P, N // 4], I32, name="w4_sc", align_bytes=64)
        zero = keep.tile([P, 1], F32, name="zero")
        no_bias = keep.tile([P, 1], F32, name="no_bias")
        b_row = keep.tile([P, N], F32, name="b_row")
        identity = keep.tile([P, P], F32, name="identity")
        nc.gpsimd.memset(tab_sc[:], 0)
        make_identity(nc, identity[:])
        nc.vector.memset(b_row[:], 0.0)
        nc.vector.memset(w4_sc[:], 0)
        nc.vector.memset(zero[:], 0.0)
        nc.scalar.activation(out=no_bias[:], in_=zero[:], func=ACT.Tanh)

        w_raw = [keep.tile([P, PACK, H], F32, name=f"w_raw{a}") for a in range(PASSES)]
        tab = [keep.tile([P, T], I32, name=f"tab{a}") for a in range(PASSES)]

        def load_tab(a):
            nc.sync.dma_start(out=tab[a][:], in_=tab_words[a].rearrange("p t i -> p (t i)").bitcast(I32))

        def load_w(a):
            nc.sync.dma_start(
                out=w_raw[a][:], in_=w1[a * K_PASS : (a + 1) * K_PASS, :].rearrange("(p j) c -> p j c", j=PACK)
            )

        load_tab(0)
        nc.sync.dma_start(offsets[:], offs)
        nc.sync.dma_start(out=b_row[0:1, :], in_=b.rearrange("(o n) -> o n", o=1))
        load_w(0)
        for q in range(QUADRANTS):
            nc.sync.dma_start(
                out=tab_sc[32 * q : 32 * q + ROWS * PASSES, :],
                in_=tab_scales[:, ROWS * q : ROWS * (q + 1), :].bitcast(I32),
            )
        load_tab(1)
        load_w(1)
        load_w(2)
        load_tab(2)
        g_planes = gT.rearrange("(p t) n -> t p n", t=PACK)
        g_all = [keep.tile([P, T], F32, name=f"g_all{t}") for t in range(PACK)]
        for t in range(PACK):
            nc.sync.dma_start(out=g_all[t][:], in_=g_planes[t])
        w4_codes = keep.tile([P, 2 * N // 4], I32, name="w4_codes", align_bytes=64)
        nc.sync.dma_start(out=w4_codes[:], in_=w4_words[0].bitcast(I32))
        for q in range(QUADRANTS):
            nc.sync.dma_start(
                out=w4_sc[32 * q : 32 * q + ROWS, :], in_=w4_scales[0, ROWS * q : ROWS * (q + 1), :].bitcast(I32)
            )

        everything = slice(0, S)
        halves = [slice(0, BANK), slice(BANK, S)]
        v_codes = keep.tile([P, PASSES, S], U32, name="v_codes", align_bytes=64)
        w_codes = keep.tile([P, PASSES, H], U32, name="w_codes", align_bytes=64)
        w_sc = {a: keep.tile([P, H], U8, name=f"w_sc{a}", align_bytes=64) for a in range(1, PASSES)}

        def gather_words(a, cols):
            nc.vector.tensor_copy(out=v_codes[:, a, cols], in_=tab[a][:].bitcast(U32).indirect(picks(cols)))

        def quantise_w(a):
            w_bf = keep.tile([P, PACK, P, PACK], BF16, name=f"w_bf{a}", align_bytes=64)
            dst = w_bf[:].rearrange("p t m j -> p m j t")
            src = w_raw[a][:].rearrange("p j (m t) -> p m j t", t=PACK)
            cut = VECTOR_SHARE[a]
            nc.vector.tensor_copy(out=dst[:, 0:cut], in_=src[:, 0:cut])
            nc.scalar.copy(out=dst[:, cut:P], in_=src[:, cut:P])
            nc.vector.quantize_mx(
                out=w_codes[:, a, :].bitcast(FP8X4),
                scales=w_sc[a][:],
                in_=w_bf[:].rearrange("p t m j -> p (t m j)"),
            )

        v_sc = keep.tile([P, S], U8, name="v_sc", align_bytes=64)
        banks = [[psum.tile([P, BANK], F32, name=f"bank{t}_{u}") for u in range(len(halves))] for t in range(PACK)]

        bias = keep.tile([P, N_TILES], F32, name="bias")
        for n in range(N_TILES):
            nc.tensor.transpose(banks[LAST][1][:, n * P : (n + 1) * P], b_row[:, n * P : (n + 1) * P], identity[:])
        nc.scalar.copy(out=bias[:], in_=banks[LAST][1][:, 0:N:P])

        gather_words(0, everything)
        nc.vector.tensor_copy(out=v_sc[:], in_=tab_sc[:].bitcast(U8).indirect(offsets[:]))
        w_sc[0] = keep.tile([P, H], U8, name="w_sc0", tag="tab_sc", align_bytes=64)
        quantise_w(0)
        gather_words(1, everything)
        quantise_w(1)
        quantise_w(2)
        for cols in halves:
            gather_words(2, cols)

        order = [(PAIR * e + t, u) for e in range(PACK // PAIR) for u in range(len(halves)) for t in range(PAIR)]
        for a in range(PASSES):
            for t, u in order:
                nc.tensor.matmul_mx(
                    out=banks[t][u][:],
                    lhsT=w_codes[:, a, t * P : (t + 1) * P].bitcast(FP8X4),
                    lhsT_scale=w_sc[a][:, t * P : (t + 1) * P],
                    rhs=v_codes[:, a, halves[u]].bitcast(FP8X4),
                    rhs_scale=v_sc[ROWS * a : P, halves[u]],
                    start=(a == 0),
                    stop=(a == PASSES - 1),
                )

        run = [WIDE] + [BANK] * LAST
        a_sb = keep.tile([P, PACK, S], F32, name="a_sb")
        for t, u in order:
            for first in range(0, BANK, run[t]):
                nc.scalar.copy(
                    out=a_sb[:, t, u * BANK + first : u * BANK + first + run[t]],
                    in_=banks[t][u][:, first : first + run[t]],
                )

        pieces = [slice(sum(WIDTHS[:i]), sum(WIDTHS[: i + 1])) for i in range(len(WIDTHS))]
        wide_end = pieces[2].stop
        h_first = PAIR * wide_end
        diff_at = [(cols.start, wide_end + cols.start) for cols in pieces[:3]]
        diff_at.extend((k * NARROW, h_first + k * NARROW) for k in range(2))
        late = keep.tile([P, PAIR * h_first + NARROW], F32, name="late", align_bytes=64)
        diff_early = keep.tile([P, PAIR, S], F32, name="diff_early")
        h_bf = [late[:, h_first : h_first + PAIR * WIDE].bitcast(BF16).rearrange("p (j t) -> p j t", t=PACK)]
        for i in range(1, len(WIDTHS)):
            h_bf.append(keep.tile([P, WIDTHS[i], PACK], BF16, name=f"h_bf{i}", align_bytes=64)[:])
        h_sc = keep.tile([P, S], U8, name="h_sc", align_bytes=64)
        result = keep.tile([P, N_TILES, S], F32, name="result")
        out_view = out.rearrange("(c p) j -> p c j", p=P)
        w4_bytes = w4_codes[:].bitcast(U8)
        w4_sc_bytes = w4_sc[:].bitcast(U8)

        def subtract(t, cols, diff):
            nc.vector.tensor_tensor(
                out=diff,
                in0=g_all[t][:].indirect(picks(cols)),
                in1=a_sb[:, t, cols],
                op=ALU.subtract,
            )

        def late_pair(i):
            first, second = diff_at[i]
            apart = second - first
            return late[:, first : first + PAIR * apart].rearrange("p (t j) -> p t j", t=PAIR)[:, :, 0 : WIDTHS[i]]

        def abs_on_scalar(i, first_plane, diff):
            nc.scalar.activation(
                out=h_bf[i][:, :, first_plane : first_plane + PAIR].rearrange("p (c i) t -> p c t i", i=LINE),
                in_=diff.rearrange("p t (c i) -> p c t i", i=LINE),
                func=ACT.Abs,
                bias=no_bias[:],
            )

        def abs_on_vector(i):
            diff = late_pair(i).rearrange("p t j -> p j t")
            nc.vector.scalar_tensor_tensor(
                out=h_bf[i][:, :, PAIR:PACK], in0=diff, scalar=-1.0, in1=diff, op0=ALU.mult, op1=ALU.max
            )

        def subtract_late(t, i, count=1):
            cols = slice(pieces[i].start, pieces[i + count - 1].stop)
            at = diff_at[i][t - PAIR]
            subtract(t, cols, late[:, at : at + cols.stop - cols.start])

        free = [banks[t][u] for t, u in order]
        places = []
        for width in WIDTHS:
            if width == WIDE:
                alone, shared = free.pop(0), free.pop(0)
                places.append([alone[:, 0:width], shared[:, 0:width], shared[:, width : 2 * width]])
            else:
                mine = free.pop(0)
                places.append([mine[:, n * width : (n + 1) * width] for n in range(N_TILES)])

        def score(i):
            h_codes = keep.tile([P, WIDTHS[i]], U32, name=f"h_codes{i}", align_bytes=64)
            nc.vector.quantize_mx(
                out=h_codes[:].bitcast(FP8X4),
                scales=h_sc[:, pieces[i]],
                in_=h_bf[i].rearrange("p j t -> p (j t)"),
            )
            for n in range(N_TILES):
                nc.tensor.matmul_mx(
                    out=places[i][n],
                    lhsT=w4_bytes[:, 2 * P * n : 2 * P * (n + 1)].bitcast(FP4X4),
                    lhsT_scale=w4_sc_bytes[:, P * n : P * (n + 1)],
                    rhs=h_codes[:].bitcast(FP8X4),
                    rhs_scale=h_sc[:, pieces[i]],
                    start=True,
                    stop=True,
                )

        def finish(i, store_after):
            cols = pieces[i]
            stored = 0
            for n in range(N_TILES):
                nc.scalar.activation(out=result[:, n, cols], in_=places[i][n], func=ACT.Tanh, bias=bias[:, n : n + 1])
                if n in store_after:
                    nc.sync.dma_start(out=out_view[:, stored : n + 1, cols], in_=result[:, stored : n + 1, cols])
                    stored = n + 1

        for t in range(PAIR):
            for first in range(0, S, run[t]):
                cols = slice(first, first + run[t])
                subtract(t, cols, diff_early[:, t, cols])
        for i, cols in enumerate(pieces):
            abs_on_scalar(i, 0, diff_early[:, :, cols])
        subtract_late(PAIR, 0, count=3)

        whole, two_parts, by_tile = (2,), (1, 2), (0, 1, 2)
        for i in range(3):
            subtract_late(LAST, i)
            abs_on_scalar(i, PAIR, late_pair(i))
        score(0)
        subtract_late(PAIR, 3, count=2)
        score(1)
        finish(0, two_parts)
        finish(1, by_tile)
        subtract_late(LAST, 3, count=2)
        score(2)
        finish(2, by_tile)
        abs_on_vector(3)
        abs_on_vector(4)
        score(3)
        score(4)
        finish(3, whole)
        finish(4, two_parts)
